import numpy as np
import ml_dtypes


def mxq(x, axis, fmt="e4m3"):
    dtype, down = {"e4m3": (ml_dtypes.float8_e4m3fn, 7), "e5m2": (ml_dtypes.float8_e5m2, 14)}[fmt]
    v = np.moveaxis(np.asarray(x, np.float32).astype(ml_dtypes.bfloat16).astype(np.float64), axis, -1)
    blocks = v.reshape(v.shape[:-1] + (-1, 32))
    amax = np.abs(blocks).max(-1, keepdims=True)
    byte = np.maximum(np.where(amax > 0, np.frexp(amax)[1] - 1 + 127, 0) - down, 1)
    scale = np.exp2(byte - 127.0)
    codes = (blocks / scale).astype(np.float32).astype(dtype).astype(np.float64)
    return np.moveaxis((codes * scale).reshape(v.shape), -1, axis)


WIDE = False


def mx_kscale(k):
    if not WIDE:
        return np.ones(k)
    levels = np.array([10, -10, 5, -5, 0])
    if k % 512:
        return np.exp2(np.random.permutation(np.resize(levels, k // 32))).repeat(32)
    a = np.empty((k // 512, 16))
    for p in range(k // 512):
        a[p, :8] = np.random.permutation(np.resize(levels, 8))
        for g in range(8):
            far = levels[np.abs(levels - a[p, g]) >= 10]
            a[p, g + 8] = far[np.random.randint(len(far))]
    return np.exp2(a.ravel()).repeat(32)


def f64(x):
    return np.asarray(x).astype(np.float64)


def striped(idx):
    return np.tile(idx.reshape(-1, 16).T, (8, 1)).astype(np.uint16)


def unstriped(offs):
    return offs[:16].T.reshape(-1).astype(np.int64)


def pack_weight(w):
    k, n = w.shape
    w = f64(np.asarray(w, np.float32).astype(ml_dtypes.bfloat16)).reshape(k // 32, 32, n)
    amax = np.abs(w).max(1)
    byte = np.clip(np.where(amax > 0, np.frexp(amax)[1] - 1 + 127 - 7, 1), 1, 254)
    scaled = (w * np.exp2(127.0 - byte)[:, None, :]).reshape(k, n).astype(np.float32)
    words = np.ascontiguousarray(scaled.reshape(k // 512, 128, 4, n).transpose(0, 1, 3, 2)).astype(ml_dtypes.float8_e4m3fn).view(np.uint8)
    return words, np.ascontiguousarray(byte.astype(np.uint8).reshape(k // 512, 16, n))


def unpack_weight(words, scales):
    g, p, n, _ = words.shape
    vals = np.ascontiguousarray(words).view(ml_dtypes.float8_e4m3fn).astype(np.float64) * np.repeat(np.exp2(scales.astype(np.float64) - 127.0), 8, axis=1)[..., None]
    return vals.transpose(0, 1, 3, 2).reshape(g * 512, n)


def sigmoid(v):
    return 1.0 / (1.0 + np.exp(-np.maximum(v, -700.0)))

def planes(y):
    n, m = y.shape
    v = y.astype(np.float32).astype(ml_dtypes.bfloat16).astype(np.float64).reshape(n // 32, 32, m)
    top = np.abs(v).max(1)
    byte = np.clip(np.where(top > 0, np.frexp(top)[1] - 1 + 127 - 7, 1), 1, 254)
    codes = (v * np.exp2(127.0 - byte)[:, None, :]).reshape(n, m).astype(np.float32).astype(ml_dtypes.float8_e4m3fn).view(np.uint8)
    words = codes.reshape(n // 512, 128, 4, m).transpose(0, 1, 3, 2)
    return np.ascontiguousarray(words), np.ascontiguousarray(byte.astype(np.uint8).reshape(n // 512, 16, m))


K, T, S, N = 512, 2048, 512, 512


def setup_inputs():
    n = np.random.standard_normal
    s = mx_kscale(K)[:, None]
    packed_xT = pack_weight(n((K, T)) * s)
    return {
        "x_words": packed_xT[0],
        "x_scales": packed_xT[1],
        "w1": (n((K, N)) / np.sqrt(K) / s).astype(np.float32),
        "w2": (n((K, N)) / np.sqrt(K) / s).astype(np.float32),
        "w3": (n((K, N)) / np.sqrt(K) / s).astype(np.float32),
        "cell": n((N, T)).astype(np.float32),
        "offs": striped(np.random.permutation(T)[(T * np.random.uniform(0, 1, S) ** 4).astype(np.int64)]),
    }


def reference(x_words, x_scales, w1, w2, w3, cell, offs):
    xq = unpack_weight(x_words, x_scales)[:, unstriped(offs)]
    f = sigmoid(mxq(f64(w1), 0, "e4m3").T @ xq)
    r = f64(cell)[:, unstriped(offs)]
    i = sigmoid(mxq(f64(w2), 0, "e4m3").T @ xq)
    g = np.tanh(mxq(f64(w3), 0, "e4m3").T @ xq)
    out_0 = f * r + i * g
    return (out_0,) + planes(out_0)

@@ -1,0 +1,169 @@
+from contextlib import ExitStack
+
+import concourse.mybir as mybir
+
+K, T, S, N = 512, 2048, 512, 512
+FLOPS = 3 * 2 * K * N * S
+
+F32 = mybir.dt.float32
+BF16 = mybir.dt.bfloat16
+I32 = mybir.dt.int32
+U32 = mybir.dt.uint32
+U16 = mybir.dt.uint16
+U8 = mybir.dt.uint8
+FP8X4 = mybir.dt.float8_e4m3fn_x4
+ACT = mybir.ActivationFunctionType
+MULT = mybir.AluOpType.mult
+ADD = mybir.AluOpType.add
+
+P = 128
+PACK = 4
+HALF = S // 2
+M_VECTOR = 80
+
+
+def tile_picked_beamcell_none_po_kernel(
+    tc, x_words, x_scales, w1, w2, w3, cell, offs, out_0, out_1, out_2
+):
+    nc = tc.nc
+    with ExitStack() as ctx:
+        sb = ctx.enter_context(tc.tile_pool(name="sb", bufs=1))
+        psum = ctx.enter_context(tc.psum_pool(name="psum", bufs=8))
+
+        offsets = sb.tile([P, S // 16], U16, name="offsets")
+        word_table = sb.tile([P, T], U32, name="word_table")
+        scale_table = sb.tile([P, T], U8, name="scale_table")
+        warm = sb.tile([P, 2], F32, name="warm")
+        raw = {}
+        for name in ("i", "g", "f"):
+            raw[name] = sb.tile([P, PACK, N], F32, name="raw_" + name)
+        cells = [sb.tile([P, T], F32, name="cell%d" % t) for t in range(PACK)]
+
+        nc.vector.memset(scale_table[:].bitcast(I32), 0)
+        nc.vector.memset(warm[:, 0:1], 0.0)
+        nc.scalar.activation(warm[:, 1:2], warm[:, 0:1], ACT.Sigmoid)
+
+        def load_w(name, w):
+            nc.sync.dma_start(raw[name][:], w.rearrange("(p j) c -> p j c", j=PACK))
+
+        load_w("i", w2)
+        nc.sync.dma_start(offsets[:], offs)
+        for q in range(4):
+            nc.sync.dma_start(
+                scale_table[32 * q : 32 * q + 4, :].bitcast(I32),
+                x_scales[0, 4 * q : 4 * q + 4, :].bitcast(I32),
+            )
+        nc.sync.dma_start(word_table[:].bitcast(I32), x_words[0].rearrange("p n r -> p (n r)").bitcast(I32))
+        load_w("g", w3)
+        load_w("f", w1)
+        cell_rows = cell.rearrange("(p t) c -> p t c", t=PACK)
+        for t in range(PACK):
+            nc.sync.dma_start(cells[t][:], cell_rows[:, t, :])
+
+        x_codes = sb.tile([P, S], U32, name="x_codes", align_bytes=64)
+        x_bytes = sb.tile([P, S], U8, name="x_bytes", align_bytes=64)
+        grouped, codes, scales = {}, {}, {}
+        for name in ("i", "g", "f"):
+            grouped[name] = sb.tile([P, PACK, P, PACK], BF16, name="grouped_" + name, align_bytes=64)
+            codes[name] = sb.tile([P, N], U32, name="codes_" + name, align_bytes=64)
+            scales[name] = sb.tile([P, N], U8, name="scales_" + name, align_bytes=64)
+
+        def deal(copy, name, m0, m1):
+            copy(
+                grouped[name][:].rearrange("p t m j -> p m j t")[:, m0:m1],
+                raw[name][:].rearrange("p j (m t) -> p m j t", t=PACK)[:, m0:m1],
+            )
+
+        def quantise(name):
+            nc.vector.quantize_mx(
+                out=codes[name][:].bitcast(FP8X4),
+                scales=scales[name][:],
+                in_=grouped[name][:].rearrange("p t m j -> p (t m j)"),
+            )
+
+        def gate(name, t, func):
+            acc = psum.tile([P, S], F32, name="acc")
+            nc.tensor.matmul_mx(
+                out=acc[:],
+                lhsT=codes[name][:, P * t : P * (t + 1)].bitcast(FP8X4),
+                lhsT_scale=scales[name][:, P * t : P * (t + 1)],
+                rhs=x_codes[:].bitcast(FP8X4),
+                rhs_scale=x_bytes[:],
+                start=True,
+                stop=True,
+            )
+            value = sb.tile([P, S], F32, name="%s%d" % (name, t))
+            nc.scalar.activation(value[:], acc[:], func)
+            return value
+
+        deal(nc.vector.tensor_copy, "i", 0, P)
+        nc.vector.tensor_copy(x_bytes[:], scale_table[:].indirect(offsets[:]))
+        quantise("i")
+        nc.vector.tensor_copy(x_codes[:], word_table[:].indirect(offsets[:]))
+        let_in = [gate("i", t, ACT.Sigmoid) for t in range(PACK)]
+        deal(nc.vector.tensor_copy, "g", 0, P)
+        quantise("g")
+        deal(nc.vector.tensor_copy, "f", 0, P)
+        quantise("f")
+
+        fresh = [sb.tile([P, S], F32, name="fresh%d" % t) for t in range(PACK)]
+        kept = [sb.tile([P, S], F32, name="kept%d" % t) for t in range(PACK)]
+        y01 = sb.tile([P, 2, S], F32, name="y01")
+        y23 = sb.tile([P, 2, 2, HALF], F32, name="y23")
+        y_bf = sb.tile([P, S, PACK], BF16, name="y_bf", align_bytes=64)
+        y_codes = sb.tile([P, S], U32, name="y_codes", align_bytes=64)
+        y_scales = sb.tile([P, S], U8, name="y_scales", align_bytes=64)
+        out_rows = out_0.rearrange("(p t) c -> p t c", t=PACK)
+        out_words = out_1[0].rearrange("p n r -> p (n r)").bitcast(I32)
+
+        new, f = {}, {}
+        for t in range(PACK):
+            new[t] = gate("g", t, ACT.Tanh)
+            f[t] = gate("f", t, ACT.Sigmoid)
+
+        def make_fresh(t):
+            nc.vector.tensor_tensor(fresh[t][:], let_in[t][:], new[t][:], MULT)
+
+        make_fresh(0)
+        for t in range(3):
+            nc.vector.tensor_tensor(kept[t][:], cells[t][:].indirect(offsets[:]), f[t][:], MULT)
+            make_fresh(t + 1)
+            if t < 2:
+                nc.vector.tensor_tensor(y01[:, t, :], kept[t][:], fresh[t][:], ADD)
+            else:
+                nc.vector.tensor_tensor(
+                    y23[:, :, 0, :],
+                    kept[t][:].rearrange("p (h c) -> p h c", h=2),
+                    fresh[t][:].rearrange("p (h c) -> p h c", h=2),
+                    ADD,
+                )
+            if t == 1:
+                nc.sync.dma_start(out_rows[:, 0:2, :], y01[:])
+                nc.scalar.copy(y_bf[:, :, 0:2], y01[:].rearrange("p t c -> p c t"))
+
+        halves = [slice(h * HALF, (h + 1) * HALF) for h in range(2)]
+        for h in range(2):
+            nc.vector.tensor_tensor(
+                kept[3][:, halves[h]],
+                cells[3][:].indirect(offsets[:, h * HALF // 16 : (h + 1) * HALF // 16]),
+                f[3][:, halves[h]],
+                MULT,
+            )
+        for h in range(2):
+            nc.vector.tensor_tensor(y23[:, h, 1, :], kept[3][:, halves[h]], fresh[3][:, halves[h]], ADD)
+            nc.sync.dma_start(out_rows[:, 2:4, halves[h]], y23[:, h])
+        nc.scalar.copy(y_bf[:, halves[0], 2:4], y23[:, 0].rearrange("p t c -> p c t"))
+        nc.vector.tensor_copy(y_bf[:, halves[1], 2:4], y23[:, 1].rearrange("p t c -> p c t"))
+        for h in range(2):
+            nc.vector.quantize_mx(
+                out=y_codes[:, halves[h]].bitcast(FP8X4),
+                scales=y_scales[:, halves[h]],
+                in_=y_bf[:, halves[h], :].rearrange("p c t -> p (c t)"),
+            )
+            nc.sync.dma_start(out_words[:, halves[h]], y_codes[:, halves[h]].bitcast(I32))
+        for q in range(4):
+            queue = nc.scalar if q % 2 == 0 else nc.sync
+            queue.dma_start(
+                out_2[0, 4 * q : 4 * q + 4, :].bitcast(I32),
+                y_scales[32 * q : 32 * q + 4, :].bitcast(I32),
+            )

@@ -19,7 +19,6 @@ ADD = mybir.AluOpType.add
 P = 128
 PACK = 4
 HALF = S // 2
-M_VECTOR = 80
 
 
 def tile_picked_beamcell_none_po_kernel(
@@ -31,8 +30,8 @@ def tile_picked_beamcell_none_po_kernel(
         psum = ctx.enter_context(tc.psum_pool(name="psum", bufs=8))
 
         offsets = sb.tile([P, S // 16], U16, name="offsets")
-        word_table = sb.tile([P, T], U32, name="word_table")
-        scale_table = sb.tile([P, T], U8, name="scale_table")
+        word_table = sb.tile([P, T], U32, name="word_table", tag="staged1", align_bytes=64)
+        scale_table = sb.tile([P, T], U8, name="scale_table", tag="staged0", align_bytes=64)
         warm = sb.tile([P, 2], F32, name="warm")
         raw = {}
         for name in ("i", "g", "f"):
@@ -46,65 +45,70 @@ def tile_picked_beamcell_none_po_kernel(
         def load_w(name, w):
             nc.sync.dma_start(raw[name][:], w.rearrange("(p j) c -> p j c", j=PACK))
 
-        load_w("i", w2)
+        word_rows = x_words[0].rearrange("p n r -> p (n r)").bitcast(I32)
+        for c0 in (0, T // 2):
+            nc.sync.dma_start(word_table[:, c0 : c0 + T // 2].bitcast(I32), word_rows[:, c0 : c0 + T // 2])
         nc.sync.dma_start(offsets[:], offs)
         for q in range(4):
             nc.sync.dma_start(
                 scale_table[32 * q : 32 * q + 4, :].bitcast(I32),
                 x_scales[0, 4 * q : 4 * q + 4, :].bitcast(I32),
             )
-        nc.sync.dma_start(word_table[:].bitcast(I32), x_words[0].rearrange("p n r -> p (n r)").bitcast(I32))
+        load_w("i", w2)
         load_w("g", w3)
         load_w("f", w1)
         cell_rows = cell.rearrange("(p t) c -> p t c", t=PACK)
         for t in range(PACK):
             nc.sync.dma_start(cells[t][:], cell_rows[:, t, :])
 
-        x_codes = sb.tile([P, S], U32, name="x_codes", align_bytes=64)
-        x_bytes = sb.tile([P, S], U8, name="x_bytes", align_bytes=64)
-        grouped, codes, scales = {}, {}, {}
-        for name in ("i", "g", "f"):
-            grouped[name] = sb.tile([P, PACK, P, PACK], BF16, name="grouped_" + name, align_bytes=64)
-            codes[name] = sb.tile([P, N], U32, name="codes_" + name, align_bytes=64)
-            scales[name] = sb.tile([P, N], U8, name="scales_" + name, align_bytes=64)
+        staged, codes, scales = {}, {}, {}
 
-        def deal(copy, name, m0, m1):
+        def deal(copy, name, u, tag):
+            staged[name, u] = sb.tile([P, 2, P, PACK], BF16, name="staged", tag=tag, align_bytes=64)
             copy(
-                grouped[name][:].rearrange("p t m j -> p m j t")[:, m0:m1],
-                raw[name][:].rearrange("p j (m t) -> p m j t", t=PACK)[:, m0:m1],
+                staged[name, u][:].rearrange("p t m j -> p m j t"),
+                raw[name][:].rearrange("p j (m t) -> p m j t", t=PACK)[:, :, :, 2 * u : 2 * u + 2],
             )
 
-        def quantise(name):
+        def quantise(name, u):
+            codes[name, u] = sb.tile([P, 2 * P], U32, name="codes_%s%d" % (name, u), align_bytes=64)
+            scales[name, u] = sb.tile([P, 2 * P], U8, name="scales_%s%d" % (name, u), align_bytes=64)
             nc.vector.quantize_mx(
-                out=codes[name][:].bitcast(FP8X4),
-                scales=scales[name][:],
-                in_=grouped[name][:].rearrange("p t m j -> p (t m j)"),
+                out=codes[name, u][:].bitcast(FP8X4),
+                scales=scales[name, u][:],
+                in_=staged[name, u][:].rearrange("p t m j -> p (t m j)"),
             )
 
         def gate(name, t, func):
+            cols = slice(P * (t % 2), P * (t % 2 + 1))
             acc = psum.tile([P, S], F32, name="acc")
             nc.tensor.matmul_mx(
                 out=acc[:],
-                lhsT=codes[name][:, P * t : P * (t + 1)].bitcast(FP8X4),
-                lhsT_scale=scales[name][:, P * t : P * (t + 1)],
+                lhsT=codes[name, t // 2][:, cols].bitcast(FP8X4),
+                lhsT_scale=scales[name, t // 2][:, cols],
                 rhs=x_codes[:].bitcast(FP8X4),
                 rhs_scale=x_bytes[:],
                 start=True,
                 stop=True,
             )
-            value = sb.tile([P, S], F32, name="%s%d" % (name, t))
+            value = sb.tile([P, S], F32, name="%s%d" % (name, t), tag="%s%d" % (name, t), align_bytes=64)
             nc.scalar.activation(value[:], acc[:], func)
             return value
 
-        deal(nc.vector.tensor_copy, "i", 0, P)
-        nc.vector.tensor_copy(x_bytes[:], scale_table[:].indirect(offsets[:]))
-        quantise("i")
+        def prepare(name):
+            for u in range(2):
+                deal(nc.vector.tensor_copy, name, u, "staged%d" % u)
+            for u in range(2):
+                quantise(name, u)
+
+        x_bytes = sb.tile([P, S], U8, name="x_bytes", align_bytes=64)
+        x_codes = sb.tile([P, S], U32, name="x_codes", align_bytes=64)
         nc.vector.tensor_copy(x_codes[:], word_table[:].indirect(offsets[:]))
+        nc.vector.tensor_copy(x_bytes[:], scale_table[:].indirect(offsets[:]))
+        prepare("i")
         let_in = [gate("i", t, ACT.Sigmoid) for t in range(PACK)]
-        deal(nc.vector.tensor_copy, "g", 0, P)
-        quantise("g")
-        deal(nc.vector.tensor_copy, "f", 0, P)
-        quantise("f")
+        prepare("g")
+        new = [gate("g", t, ACT.Tanh) for t in range(3)]
 
         fresh = [sb.tile([P, S], F32, name="fresh%d" % t) for t in range(PACK)]
         kept = [sb.tile([P, S], F32, name="kept%d" % t) for t in range(PACK)]
@@ -116,37 +120,40 @@ def tile_picked_beamcell_none_po_kernel(
         out_rows = out_0.rearrange("(p t) c -> p t c", t=PACK)
         out_words = out_1[0].rearrange("p n r -> p (n r)").bitcast(I32)
 
-        new, f = {}, {}
-        for t in range(PACK):
-            new[t] = gate("g", t, ACT.Tanh)
-            f[t] = gate("f", t, ACT.Sigmoid)
-
         def make_fresh(t):
             nc.vector.tensor_tensor(fresh[t][:], let_in[t][:], new[t][:], MULT)
 
+        def make_kept(t):
+            nc.vector.tensor_tensor(kept[t][:], cells[t][:].indirect(offsets[:]), keep[t][:], MULT)
+
+        prepare("f")
+        keep = [gate("f", t, ACT.Sigmoid) for t in range(2)]
+        new.append(gate("g", 3, ACT.Tanh))
+        keep.extend([gate("f", t, ACT.Sigmoid) for t in (2, 3)])
         make_fresh(0)
-        for t in range(3):
-            nc.vector.tensor_tensor(kept[t][:], cells[t][:].indirect(offsets[:]), f[t][:], MULT)
-            make_fresh(t + 1)
-            if t < 2:
-                nc.vector.tensor_tensor(y01[:, t, :], kept[t][:], fresh[t][:], ADD)
-            else:
-                nc.vector.tensor_tensor(
-                    y23[:, :, 0, :],
-                    kept[t][:].rearrange("p (h c) -> p h c", h=2),
-                    fresh[t][:].rearrange("p (h c) -> p h c", h=2),
-                    ADD,
-                )
-            if t == 1:
-                nc.sync.dma_start(out_rows[:, 0:2, :], y01[:])
-                nc.scalar.copy(y_bf[:, :, 0:2], y01[:].rearrange("p t c -> p c t"))
+        make_fresh(1)
+        make_kept(0)
+        make_fresh(2)
+        nc.vector.tensor_tensor(y01[:, 0, :], kept[0][:], fresh[0][:], ADD)
+        make_kept(1)
+        make_fresh(3)
+        nc.vector.tensor_tensor(y01[:, 1, :], kept[1][:], fresh[1][:], ADD)
+        nc.sync.dma_start(out_rows[:, 0:2, :], y01[:])
+        nc.scalar.copy(y_bf[:, :, 0:2], y01[:].rearrange("p t c -> p c t"))
+        make_kept(2)
+        nc.vector.tensor_tensor(
+            y23[:, :, 0, :],
+            kept[2][:].rearrange("p (h c) -> p h c", h=2),
+            fresh[2][:].rearrange("p (h c) -> p h c", h=2),
+            ADD,
+        )
 
         halves = [slice(h * HALF, (h + 1) * HALF) for h in range(2)]
         for h in range(2):
             nc.vector.tensor_tensor(
                 kept[3][:, halves[h]],
                 cells[3][:].indirect(offsets[:, h * HALF // 16 : (h + 1) * HALF // 16]),
-                f[3][:, halves[h]],
+                keep[3][:, halves[h]],
                 MULT,
             )
         for h in range(2):

@@ -19,6 +19,7 @@ ADD = mybir.AluOpType.add
 P = 128
 PACK = 4
 HALF = S // 2
+QUARTER = S // 4
 
 
 def tile_picked_beamcell_none_po_kernel(
@@ -105,7 +106,10 @@ def tile_picked_beamcell_none_po_kernel(
         x_codes = sb.tile([P, S], U32, name="x_codes", align_bytes=64)
         nc.vector.tensor_copy(x_codes[:], word_table[:].indirect(offsets[:]))
         nc.vector.tensor_copy(x_bytes[:], scale_table[:].indirect(offsets[:]))
-        prepare("i")
+        deal(nc.vector.tensor_copy, "i", 0, "staged0")
+        deal(nc.scalar.copy, "i", 1, "staged1")
+        for u in range(2):
+            quantise("i", u)
         let_in = [gate("i", t, ACT.Sigmoid) for t in range(PACK)]
         prepare("g")
         new = [gate("g", t, ACT.Tanh) for t in range(3)]
@@ -123,51 +127,73 @@ def tile_picked_beamcell_none_po_kernel(
         def make_fresh(t):
             nc.vector.tensor_tensor(fresh[t][:], let_in[t][:], new[t][:], MULT)
 
-        def make_kept(t):
-            nc.vector.tensor_tensor(kept[t][:], cells[t][:].indirect(offsets[:]), keep[t][:], MULT)
+        def make_kept(t, c0, c1):
+            nc.vector.tensor_tensor(
+                kept[t][:, c0:c1], cells[t][:].indirect(offsets[:, c0 // 16 : c1 // 16]), keep[t][:, c0:c1], MULT
+            )
 
-        prepare("f")
-        keep = [gate("f", t, ACT.Sigmoid) for t in range(2)]
+        def add(t, c0, c1):
+            if t < 2:
+                y = y01[:, t, c0:c1]
+            else:
+                h = c0 // HALF
+                y = y23[:, h, t - 2, c0 - h * HALF : c1 - h * HALF]
+            nc.vector.tensor_tensor(y, kept[t][:, c0:c1], fresh[t][:, c0:c1], ADD)
+
+        def combine(t):
+            for c0 in (0, HALF):
+                make_kept(t, c0, c0 + HALF)
+            for c0 in (0, HALF):
+                add(t, c0, c0 + HALF)
+
+        deal(nc.vector.tensor_copy, "f", 0, "staged0")
+        quantise("f", 0)
+        for t in range(3):
+            make_fresh(t)
+        keep = [gate("f", 0, ACT.Sigmoid)]
+        deal(nc.scalar.copy, "f", 1, "i1")
+        keep.append(gate("f", 1, ACT.Sigmoid))
         new.append(gate("g", 3, ACT.Tanh))
+        combine(0)
+        quantise("f", 1)
         keep.extend([gate("f", t, ACT.Sigmoid) for t in (2, 3)])
-        make_fresh(0)
-        make_fresh(1)
-        make_kept(0)
-        make_fresh(2)
-        nc.vector.tensor_tensor(y01[:, 0, :], kept[0][:], fresh[0][:], ADD)
-        make_kept(1)
-        make_fresh(3)
-        nc.vector.tensor_tensor(y01[:, 1, :], kept[1][:], fresh[1][:], ADD)
+        combine(1)
         nc.sync.dma_start(out_rows[:, 0:2, :], y01[:])
         nc.scalar.copy(y_bf[:, :, 0:2], y01[:].rearrange("p t c -> p c t"))
-        make_kept(2)
-        nc.vector.tensor_tensor(
-            y23[:, :, 0, :],
-            kept[2][:].rearrange("p (h c) -> p h c", h=2),
-            fresh[2][:].rearrange("p (h c) -> p h c", h=2),
-            ADD,
-        )
+        make_fresh(3)
+        combine(2)
+
+        def round_pair(copy, n):
+            h, c0 = divmod(n * QUARTER, HALF)
+            copy(
+                y_bf[:, n * QUARTER : (n + 1) * QUARTER, 2:4],
+                y23[:, h, :, c0 : c0 + QUARTER].rearrange("p t c -> p c t"),
+            )
+
+        def quantise_y(n):
+            cols = slice(n * QUARTER, (n + 1) * QUARTER)
+            nc.vector.quantize_mx(
+                out=y_codes[:, cols].bitcast(FP8X4),
+                scales=y_scales[:, cols],
+                in_=y_bf[:, cols, :].rearrange("p c t -> p (c t)"),
+            )
 
         halves = [slice(h * HALF, (h + 1) * HALF) for h in range(2)]
-        for h in range(2):
-            nc.vector.tensor_tensor(
-                kept[3][:, halves[h]],
-                cells[3][:].indirect(offsets[:, h * HALF // 16 : (h + 1) * HALF // 16]),
-                keep[3][:, halves[h]],
-                MULT,
-            )
-        for h in range(2):
-            nc.vector.tensor_tensor(y23[:, h, 1, :], kept[3][:, halves[h]], fresh[3][:, halves[h]], ADD)
-            nc.sync.dma_start(out_rows[:, 2:4, halves[h]], y23[:, h])
-        nc.scalar.copy(y_bf[:, halves[0], 2:4], y23[:, 0].rearrange("p t c -> p c t"))
-        nc.vector.tensor_copy(y_bf[:, halves[1], 2:4], y23[:, 1].rearrange("p t c -> p c t"))
-        for h in range(2):
-            nc.vector.quantize_mx(
-                out=y_codes[:, halves[h]].bitcast(FP8X4),
-                scales=y_scales[:, halves[h]],
-                in_=y_bf[:, halves[h], :].rearrange("p c t -> p (c t)"),
-            )
-            nc.sync.dma_start(out_words[:, halves[h]], y_codes[:, halves[h]].bitcast(I32))
+        make_kept(3, 0, QUARTER)
+        for n in range(4):
+            if n < 3:
+                make_kept(3, (n + 1) * QUARTER, (n + 2) * QUARTER)
+            add(3, n * QUARTER, (n + 1) * QUARTER)
+            if n < 3:
+                round_pair(nc.scalar.copy, n)
+            if n % 2 == 1:
+                nc.sync.dma_start(out_rows[:, 2:4, halves[n // 2]], y23[:, n // 2])
+        quantise_y(0)
+        round_pair(nc.vector.tensor_copy, 3)
+        for n in range(1, 4):
+            quantise_y(n)
+            if n % 2 == 1:
+                nc.sync.dma_start(out_words[:, halves[n // 2]], y_codes[:, halves[n // 2]].bitcast(I32))
         for q in range(4):
             queue = nc.scalar if q % 2 == 0 else nc.sync
             queue.dma_start(

@@ -162,6 +162,7 @@ def tile_picked_beamcell_none_po_kernel(
         nc.scalar.copy(y_bf[:, :, 0:2], y01[:].rearrange("p t c -> p c t"))
         make_fresh(3)
         combine(2)
+        nc.sync.dma_start(out_rows[:, 2, :].rearrange("p (h c) -> p h c", h=2), y23[:, :, 0, :])
 
         def round_pair(copy, n):
             h, c0 = divmod(n * QUARTER, HALF)
@@ -187,15 +188,15 @@ def tile_picked_beamcell_none_po_kernel(
             if n < 3:
                 round_pair(nc.scalar.copy, n)
             if n % 2 == 1:
-                nc.sync.dma_start(out_rows[:, 2:4, halves[n // 2]], y23[:, n // 2])
+                nc.sync.dma_start(out_rows[:, 3, halves[n // 2]], y23[:, n // 2, 1, :])
         quantise_y(0)
         round_pair(nc.vector.tensor_copy, 3)
         for n in range(1, 4):
             quantise_y(n)
             if n % 2 == 1:
-                nc.sync.dma_start(out_words[:, halves[n // 2]], y_codes[:, halves[n // 2]].bitcast(I32))
+                nc.scalar.dma_start(out_words[:, halves[n // 2]], y_codes[:, halves[n // 2]].bitcast(I32))
         for q in range(4):
-            queue = nc.scalar if q % 2 == 0 else nc.sync
+            queue = nc.scalar if q == 3 else nc.sync
             queue.dma_start(
                 out_2[0, 4 * q : 4 * q + 4, :].bitcast(I32),
                 y_scales[32 * q : 32 * q + 4, :].bitcast(I32),

@@ -28,7 +28,7 @@ def tile_picked_beamcell_none_po_kernel(
     nc = tc.nc
     with ExitStack() as ctx:
         sb = ctx.enter_context(tc.tile_pool(name="sb", bufs=1))
-        psum = ctx.enter_context(tc.psum_pool(name="psum", bufs=8))
+        psum = ctx.enter_context(tc.psum_pool(name="psum", bufs=1))
 
         offsets = sb.tile([P, S // 16], U16, name="offsets")
         word_table = sb.tile([P, T], U32, name="word_table", tag="staged1", align_bytes=64)
@@ -71,8 +71,10 @@ def tile_picked_beamcell_none_po_kernel(
                 raw[name][:].rearrange("p j (m t) -> p m j t", t=PACK)[:, :, :, 2 * u : 2 * u + 2],
             )
 
-        def quantise(name, u):
-            codes[name, u] = sb.tile([P, 2 * P], U32, name="codes_%s%d" % (name, u), align_bytes=64)
+        def quantise(name, u, tag=None):
+            codes[name, u] = sb.tile(
+                [P, 2 * P], U32, name="codes", tag=tag or "codes_%s%d" % (name, u), align_bytes=64
+            )
             scales[name, u] = sb.tile([P, 2 * P], U8, name="scales_%s%d" % (name, u), align_bytes=64)
             nc.vector.quantize_mx(
                 out=codes[name, u][:].bitcast(FP8X4),
@@ -80,20 +82,23 @@ def tile_picked_beamcell_none_po_kernel(
                 in_=staged[name, u][:].rearrange("p t m j -> p (t m j)"),
             )
 
-        def gate(name, t, func):
+        def gate(name, t, func, *banks):
             cols = slice(P * (t % 2), P * (t % 2 + 1))
-            acc = psum.tile([P, S], F32, name="acc")
-            nc.tensor.matmul_mx(
-                out=acc[:],
-                lhsT=codes[name, t // 2][:, cols].bitcast(FP8X4),
-                lhsT_scale=scales[name, t // 2][:, cols],
-                rhs=x_codes[:].bitcast(FP8X4),
-                rhs_scale=x_bytes[:],
-                start=True,
-                stop=True,
-            )
             value = sb.tile([P, S], F32, name="%s%d" % (name, t), tag="%s%d" % (name, t), align_bytes=64)
-            nc.scalar.activation(value[:], acc[:], func)
+            width = S // len(banks)
+            for n, bank in enumerate(banks):
+                beams = slice(n * width, (n + 1) * width)
+                acc = psum.tile([P, S], F32, name="acc", tag="bank%d" % bank)
+                nc.tensor.matmul_mx(
+                    out=acc[:, 0:width],
+                    lhsT=codes[name, t // 2][:, cols].bitcast(FP8X4),
+                    lhsT_scale=scales[name, t // 2][:, cols],
+                    rhs=x_codes[:, beams].bitcast(FP8X4),
+                    rhs_scale=x_bytes[:, beams],
+                    start=True,
+                    stop=True,
+                )
+                nc.scalar.activation(value[:, beams], acc[:, 0:width], func)
             return value
 
         def prepare(name):
@@ -110,9 +115,11 @@ def tile_picked_beamcell_none_po_kernel(
         deal(nc.scalar.copy, "i", 1, "staged1")
         for u in range(2):
             quantise("i", u)
-        let_in = [gate("i", t, ACT.Sigmoid) for t in range(PACK)]
+        let_in = [gate("i", t, ACT.Sigmoid, t) for t in range(3)]
         prepare("g")
-        new = [gate("g", t, ACT.Tanh) for t in range(3)]
+        new = {}
+        for t, bank in ((0, 3), (2, 4), (1, 3)):
+            new[t] = gate("g", t, ACT.Tanh, bank)
 
         fresh = [sb.tile([P, S], F32, name="fresh%d" % t) for t in range(PACK)]
         kept = [sb.tile([P, S], F32, name="kept%d" % t) for t in range(PACK)]
@@ -140,29 +147,28 @@ def tile_picked_beamcell_none_po_kernel(
                 y = y23[:, h, t - 2, c0 - h * HALF : c1 - h * HALF]
             nc.vector.tensor_tensor(y, kept[t][:, c0:c1], fresh[t][:, c0:c1], ADD)
 
-        def combine(t):
-            for c0 in (0, HALF):
-                make_kept(t, c0, c0 + HALF)
-            for c0 in (0, HALF):
-                add(t, c0, c0 + HALF)
-
         deal(nc.vector.tensor_copy, "f", 0, "staged0")
-        quantise("f", 0)
-        for t in range(3):
-            make_fresh(t)
-        keep = [gate("f", 0, ACT.Sigmoid)]
-        deal(nc.scalar.copy, "f", 1, "i1")
-        keep.append(gate("f", 1, ACT.Sigmoid))
-        new.append(gate("g", 3, ACT.Tanh))
-        combine(0)
+        make_fresh(0)
+        quantise("f", 0, "codes_g0")
+        make_fresh(2)
+        make_fresh(1)
+        keep = [gate("f", 0, ACT.Sigmoid, 5, 7), gate("f", 1, ACT.Sigmoid, 6)]
+        deal(nc.scalar.copy, "f", 1, "codes_g0")
+        let_in.append(gate("i", 3, ACT.Sigmoid, 6))
+        new[3] = gate("g", 3, ACT.Tanh, 5)
+        make_kept(0, 0, HALF)
+        make_kept(0, HALF, S)
+        add(0, 0, HALF)
+        add(0, HALF, S)
         quantise("f", 1)
-        keep.extend([gate("f", t, ACT.Sigmoid) for t in (2, 3)])
-        combine(1)
+        keep.extend([gate("f", t, ACT.Sigmoid, t - 2) for t in (2, 3)])
+        make_kept(1, 0, S)
+        make_fresh(3)
+        add(1, 0, S)
         nc.sync.dma_start(out_rows[:, 0:2, :], y01[:])
         nc.scalar.copy(y_bf[:, :, 0:2], y01[:].rearrange("p t c -> p c t"))
-        make_fresh(3)
-        combine(2)
-        nc.sync.dma_start(out_rows[:, 2, :].rearrange("p (h c) -> p h c", h=2), y23[:, :, 0, :])
+        make_kept(2, 0, HALF)
+        make_kept(2, HALF, S)
 
         def round_pair(copy, n):
             h, c0 = divmod(n * QUARTER, HALF)
@@ -180,6 +186,9 @@ def tile_picked_beamcell_none_po_kernel(
             )
 
         halves = [slice(h * HALF, (h + 1) * HALF) for h in range(2)]
+        add(2, 0, HALF)
+        add(2, HALF, S)
+        nc.sync.dma_start(out_rows[:, 2, :].rearrange("p (h c) -> p h c", h=2), y23[:, :, 0, :])
         make_kept(3, 0, QUARTER)
         for n in range(4):
             if n < 3:

@@ -50,10 +50,10 @@ def tile_picked_beamcell_none_po_kernel(
         for c0 in (0, T // 2):
             nc.sync.dma_start(word_table[:, c0 : c0 + T // 2].bitcast(I32), word_rows[:, c0 : c0 + T // 2])
         nc.sync.dma_start(offsets[:], offs)
-        for q in range(4):
+        for r in range(4):
             nc.sync.dma_start(
-                scale_table[32 * q : 32 * q + 4, :].bitcast(I32),
-                x_scales[0, 4 * q : 4 * q + 4, :].bitcast(I32),
+                scale_table[r:P:32, :].bitcast(I32),
+                x_scales[0, r:16:4, :].bitcast(I32),
             )
         load_w("i", w2)
         load_w("g", w3)
@@ -82,24 +82,27 @@ def tile_picked_beamcell_none_po_kernel(
                 in_=staged[name, u][:].rearrange("p t m j -> p (t m j)"),
             )
 
-        def gate(name, t, func, *banks):
+        def product(name, t, bank, c0=0, c1=S):
             cols = slice(P * (t % 2), P * (t % 2 + 1))
-            value = sb.tile([P, S], F32, name="%s%d" % (name, t), tag="%s%d" % (name, t), align_bytes=64)
-            width = S // len(banks)
-            for n, bank in enumerate(banks):
-                beams = slice(n * width, (n + 1) * width)
-                acc = psum.tile([P, S], F32, name="acc", tag="bank%d" % bank)
-                nc.tensor.matmul_mx(
-                    out=acc[:, 0:width],
-                    lhsT=codes[name, t // 2][:, cols].bitcast(FP8X4),
-                    lhsT_scale=scales[name, t // 2][:, cols],
-                    rhs=x_codes[:, beams].bitcast(FP8X4),
-                    rhs_scale=x_bytes[:, beams],
-                    start=True,
-                    stop=True,
-                )
-                nc.scalar.activation(value[:, beams], acc[:, 0:width], func)
+            acc = psum.tile([P, c1 - c0], F32, name="acc", tag="bank%d" % bank)
+            nc.tensor.matmul_mx(
+                out=acc[:],
+                lhsT=codes[name, t // 2][:, cols].bitcast(FP8X4),
+                lhsT_scale=scales[name, t // 2][:, cols],
+                rhs=x_codes[:, c0:c1].bitcast(FP8X4),
+                rhs_scale=x_bytes[:, c0:c1],
+                start=True,
+                stop=True,
+            )
+            return acc
+
+        def activate(acc, func, tag):
+            value = sb.tile(list(acc.shape), F32, name="value", tag=tag, align_bytes=64)
+            nc.scalar.activation(value[:], acc[:], func)
             return value
+
+        def gate(name, t, func, bank):
+            return activate(product(name, t, bank), func, "%s%d" % (name, t))
 
         def prepare(name):
             for u in range(2):
@@ -134,9 +137,12 @@ def tile_picked_beamcell_none_po_kernel(
         def make_fresh(t):
             nc.vector.tensor_tensor(fresh[t][:], let_in[t][:], new[t][:], MULT)
 
-        def make_kept(t, c0, c1):
+        def make_kept(t, c0, c1, factor=None):
             nc.vector.tensor_tensor(
-                kept[t][:, c0:c1], cells[t][:].indirect(offsets[:, c0 // 16 : c1 // 16]), keep[t][:, c0:c1], MULT
+                kept[t][:, c0:c1],
+                cells[t][:].indirect(offsets[:, c0 // 16 : c1 // 16]),
+                keep[t][:, c0:c1] if factor is None else factor[:],
+                MULT,
             )
 
         def add(t, c0, c1):
@@ -152,16 +158,22 @@ def tile_picked_beamcell_none_po_kernel(
         quantise("f", 0, "codes_g0")
         make_fresh(2)
         make_fresh(1)
-        keep = [gate("f", 0, ACT.Sigmoid, 5, 7), gate("f", 1, ACT.Sigmoid, 6)]
+        f0 = [
+            activate(product("f", 0, bank, h * HALF, (h + 1) * HALF), ACT.Sigmoid, "f0_%d" % h)
+            for h, bank in enumerate((5, 7))
+        ]
+        acc_f1 = product("f", 1, 6)
         deal(nc.scalar.copy, "f", 1, "codes_g0")
-        let_in.append(gate("i", 3, ACT.Sigmoid, 6))
+        keep = {1: activate(acc_f1, ACT.Sigmoid, "f1")}
+        let_in.append(gate("i", 3, ACT.Sigmoid, 7))
         new[3] = gate("g", 3, ACT.Tanh, 5)
-        make_kept(0, 0, HALF)
-        make_kept(0, HALF, S)
+        for h in range(2):
+            make_kept(0, h * HALF, (h + 1) * HALF, f0[h])
         add(0, 0, HALF)
         add(0, HALF, S)
-        quantise("f", 1)
-        keep.extend([gate("f", t, ACT.Sigmoid, t - 2) for t in (2, 3)])
+        quantise("f", 1, "f0_1")
+        for t in (2, 3):
+            keep[t] = gate("f", t, ACT.Sigmoid, t - 2)
         make_kept(1, 0, S)
         make_fresh(3)
         add(1, 0, S)

@@ -44,11 +44,12 @@ def tile_picked_beamcell_none_po_kernel(
         nc.scalar.activation(warm[:, 1:2], warm[:, 0:1], ACT.Sigmoid)
 
         def load_w(name, w):
-            nc.sync.dma_start(raw[name][:], w.rearrange("(p j) c -> p j c", j=PACK))
+            nc.sync.dma_start(
+                raw[name][:].rearrange("p j c -> p (j c)"), w.rearrange("(p j) c -> p (j c)", j=PACK)
+            )
 
         word_rows = x_words[0].rearrange("p n r -> p (n r)").bitcast(I32)
-        for c0 in (0, T // 2):
-            nc.sync.dma_start(word_table[:, c0 : c0 + T // 2].bitcast(I32), word_rows[:, c0 : c0 + T // 2])
+        nc.sync.dma_start(word_table[:].bitcast(I32), word_rows)
         nc.sync.dma_start(offsets[:], offs)
         for r in range(4):
             nc.sync.dma_start(
@@ -127,7 +128,7 @@ def tile_picked_beamcell_none_po_kernel(
         fresh = [sb.tile([P, S], F32, name="fresh%d" % t) for t in range(PACK)]
         kept = [sb.tile([P, S], F32, name="kept%d" % t) for t in range(PACK)]
         y01 = sb.tile([P, 2, S], F32, name="y01")
-        y23 = sb.tile([P, 2, 2, HALF], F32, name="y23")
+        y23 = sb.tile([P, 2, S], F32, name="y23")
         y_bf = sb.tile([P, S, PACK], BF16, name="y_bf", align_bytes=64)
         y_codes = sb.tile([P, S], U32, name="y_codes", align_bytes=64)
         y_scales = sb.tile([P, S], U8, name="y_scales", align_bytes=64)
@@ -146,11 +147,7 @@ def tile_picked_beamcell_none_po_kernel(
             )
 
         def add(t, c0, c1):
-            if t < 2:
-                y = y01[:, t, c0:c1]
-            else:
-                h = c0 // HALF
-                y = y23[:, h, t - 2, c0 - h * HALF : c1 - h * HALF]
+            y = (y01 if t < 2 else y23)[:, t % 2, c0:c1]
             nc.vector.tensor_tensor(y, kept[t][:, c0:c1], fresh[t][:, c0:c1], ADD)
 
         deal(nc.vector.tensor_copy, "f", 0, "staged0")
@@ -182,12 +179,8 @@ def tile_picked_beamcell_none_po_kernel(
         make_kept(2, 0, HALF)
         make_kept(2, HALF, S)
 
-        def round_pair(copy, n):
-            h, c0 = divmod(n * QUARTER, HALF)
-            copy(
-                y_bf[:, n * QUARTER : (n + 1) * QUARTER, 2:4],
-                y23[:, h, :, c0 : c0 + QUARTER].rearrange("p t c -> p c t"),
-            )
+        def round_pair(copy, c0, c1):
+            copy(y_bf[:, c0:c1, 2:4], y23[:, :, c0:c1].rearrange("p t c -> p c t"))
 
         def quantise_y(n):
             cols = slice(n * QUARTER, (n + 1) * QUARTER)
@@ -200,18 +193,18 @@ def tile_picked_beamcell_none_po_kernel(
         halves = [slice(h * HALF, (h + 1) * HALF) for h in range(2)]
         add(2, 0, HALF)
         add(2, HALF, S)
-        nc.sync.dma_start(out_rows[:, 2, :].rearrange("p (h c) -> p h c", h=2), y23[:, :, 0, :])
+        nc.sync.dma_start(out_rows[:, 2, :], y23[:, 0, :])
         make_kept(3, 0, QUARTER)
         for n in range(4):
             if n < 3:
                 make_kept(3, (n + 1) * QUARTER, (n + 2) * QUARTER)
             add(3, n * QUARTER, (n + 1) * QUARTER)
             if n < 3:
-                round_pair(nc.scalar.copy, n)
+                round_pair(nc.scalar.copy, n * QUARTER, (n + 1) * QUARTER)
             if n % 2 == 1:
-                nc.sync.dma_start(out_rows[:, 3, halves[n // 2]], y23[:, n // 2, 1, :])
+                nc.sync.dma_start(out_rows[:, 3, halves[n // 2]], y23[:, 1, halves[n // 2]])
         quantise_y(0)
-        round_pair(nc.vector.tensor_copy, 3)
+        round_pair(nc.vector.tensor_copy, 3 * QUARTER, S)
         for n in range(1, 4):
             quantise_y(n)
             if n % 2 == 1:

@@ -194,21 +194,35 @@ def tile_picked_beamcell_none_po_kernel(
         add(2, 0, HALF)
         add(2, HALF, S)
         nc.sync.dma_start(out_rows[:, 2, :], y23[:, 0, :])
-        make_kept(3, 0, QUARTER)
-        for n in range(4):
-            if n < 3:
-                make_kept(3, (n + 1) * QUARTER, (n + 2) * QUARTER)
-            add(3, n * QUARTER, (n + 1) * QUARTER)
-            if n < 3:
-                round_pair(nc.scalar.copy, n * QUARTER, (n + 1) * QUARTER)
+        quarters = [slice(n * QUARTER, (n + 1) * QUARTER) for n in range(4)]
+        kept_last = [kept[3][:, quarters[0]], kept[3][:, quarters[1]], keep[3][:, quarters[0]], keep[3][:, quarters[1]]]
+
+        def gather_last(n):
+            nc.vector.tensor_tensor(
+                kept_last[n],
+                cells[3][:].indirect(offsets[:, n * QUARTER // 16 : (n + 1) * QUARTER // 16]),
+                keep[3][:, quarters[n]],
+                MULT,
+            )
+
+        def add_last(n):
+            nc.vector.tensor_tensor(y23[:, 1, quarters[n]], kept_last[n], fresh[3][:, quarters[n]], ADD)
             if n % 2 == 1:
                 nc.sync.dma_start(out_rows[:, 3, halves[n // 2]], y23[:, 1, halves[n // 2]])
+
+        gather_last(0)
+        for n in range(3):
+            gather_last(n + 1)
+            add_last(n)
+            round_pair(nc.scalar.copy, n * QUARTER, (n + 1) * QUARTER)
         quantise_y(0)
+        add_last(3)
+        quantise_y(1)
+        nc.sync.dma_start(out_words[:, halves[0]], y_codes[:, halves[0]].bitcast(I32))
         round_pair(nc.vector.tensor_copy, 3 * QUARTER, S)
-        for n in range(1, 4):
-            quantise_y(n)
-            if n % 2 == 1:
-                nc.scalar.dma_start(out_words[:, halves[n // 2]], y_codes[:, halves[n // 2]].bitcast(I32))
+        quantise_y(2)
+        quantise_y(3)
+        nc.scalar.dma_start(out_words[:, halves[1]], y_codes[:, halves[1]].bitcast(I32))
         for q in range(4):
             queue = nc.scalar if q == 3 else nc.sync
             queue.dma_start(

@@ -49,7 +49,8 @@ def tile_picked_beamcell_none_po_kernel(
             )
 
         word_rows = x_words[0].rearrange("p n r -> p (n r)").bitcast(I32)
-        nc.sync.dma_start(word_table[:].bitcast(I32), word_rows)
+        for c0 in (0, T // 2):
+            nc.sync.dma_start(word_table[:, c0 : c0 + T // 2].bitcast(I32), word_rows[:, c0 : c0 + T // 2])
         nc.sync.dma_start(offsets[:], offs)
         for r in range(4):
             nc.sync.dma_start(
@@ -218,7 +219,7 @@ def tile_picked_beamcell_none_po_kernel(
         quantise_y(0)
         add_last(3)
         quantise_y(1)
-        nc.sync.dma_start(out_words[:, halves[0]], y_codes[:, halves[0]].bitcast(I32))
+        nc.scalar.dma_start(out_words[:, halves[0]], y_codes[:, halves[0]].bitcast(I32))
         round_pair(nc.vector.tensor_copy, 3 * QUARTER, S)
         quantise_y(2)
         quantise_y(3)

@@ -172,11 +172,13 @@ def tile_picked_beamcell_none_po_kernel(
         quantise("f", 1, "f0_1")
         for t in (2, 3):
             keep[t] = gate("f", t, ACT.Sigmoid, t - 2)
-        make_kept(1, 0, S)
-        make_fresh(3)
-        add(1, 0, S)
+        make_kept(1, 0, HALF)
+        make_kept(1, HALF, S)
+        for c0 in (0, HALF):
+            add(1, c0, c0 + HALF)
+            nc.scalar.copy(y_bf[:, c0 : c0 + HALF, 0:2], y01[:, :, c0 : c0 + HALF].rearrange("p t c -> p c t"))
         nc.sync.dma_start(out_rows[:, 0:2, :], y01[:])
-        nc.scalar.copy(y_bf[:, :, 0:2], y01[:].rearrange("p t c -> p c t"))
+        make_fresh(3)
         make_kept(2, 0, HALF)
         make_kept(2, HALF, S)
 
@@ -196,31 +198,45 @@ def tile_picked_beamcell_none_po_kernel(
         add(2, HALF, S)
         nc.sync.dma_start(out_rows[:, 2, :], y23[:, 0, :])
         quarters = [slice(n * QUARTER, (n + 1) * QUARTER) for n in range(4)]
-        kept_last = [kept[3][:, quarters[0]], kept[3][:, quarters[1]], keep[3][:, quarters[0]], keep[3][:, quarters[1]]]
+        picked = sb.tile([P, 2, QUARTER], F32, name="picked")
 
-        def gather_last(n):
-            nc.vector.tensor_tensor(
-                kept_last[n],
-                cells[3][:].indirect(offsets[:, n * QUARTER // 16 : (n + 1) * QUARTER // 16]),
-                keep[3][:, quarters[n]],
-                MULT,
-            )
+        def list_quarter(n):
+            return offsets[:, n * QUARTER // 16 : (n + 1) * QUARTER // 16]
+
+        def gather_times_keep(n):
+            nc.vector.tensor_tensor(kept[3][:, quarters[n]], cells[3][:].indirect(list_quarter(n)), keep[3][:, quarters[n]], MULT)
+
+        def gather_on_scalar(n):
+            nc.scalar.activation(picked[:, n - 1, :], cells[3][:].indirect(list_quarter(n)), ACT.Copy)
+
+        def times_keep(n):
+            nc.vector.tensor_tensor(kept[3][:, quarters[n]], picked[:, n - 1, :], keep[3][:, quarters[n]], MULT)
 
         def add_last(n):
-            nc.vector.tensor_tensor(y23[:, 1, quarters[n]], kept_last[n], fresh[3][:, quarters[n]], ADD)
-            if n % 2 == 1:
-                nc.sync.dma_start(out_rows[:, 3, halves[n // 2]], y23[:, 1, halves[n // 2]])
+            add(3, n * QUARTER, (n + 1) * QUARTER)
 
-        gather_last(0)
-        for n in range(3):
-            gather_last(n + 1)
-            add_last(n)
-            round_pair(nc.scalar.copy, n * QUARTER, (n + 1) * QUARTER)
-        quantise_y(0)
+        def round_last(copy, n):
+            round_pair(copy, n * QUARTER, (n + 1) * QUARTER)
+
+        gather_on_scalar(1)
+        gather_on_scalar(2)
+        gather_times_keep(0)
+        gather_times_keep(3)
+        times_keep(1)
+        add_last(0)
+        round_last(nc.scalar.copy, 0)
+        times_keep(2)
+        add_last(1)
+        nc.sync.dma_start(out_rows[:, 3, halves[0]], y23[:, 1, halves[0]])
         add_last(3)
+        round_last(nc.scalar.copy, 3)
+        add_last(2)
+        nc.sync.dma_start(out_rows[:, 3, halves[1]], y23[:, 1, halves[1]])
+        round_last(nc.vector.tensor_copy, 1)
+        round_last(nc.vector.tensor_copy, 2)
+        quantise_y(0)
         quantise_y(1)
         nc.scalar.dma_start(out_words[:, halves[0]], y_codes[:, halves[0]].bitcast(I32))
-        round_pair(nc.vector.tensor_copy, 3 * QUARTER, S)
         quantise_y(2)
         quantise_y(3)
         nc.scalar.dma_start(out_words[:, halves[1]], y_codes[:, halves[1]].bitcast(I32))

@@ -37,7 +37,7 @@ def tile_picked_beamcell_none_po_kernel(
         raw = {}
         for name in ("i", "g", "f"):
             raw[name] = sb.tile([P, PACK, N], F32, name="raw_" + name)
-        cells = [sb.tile([P, T], F32, name="cell%d" % t) for t in range(PACK)]
+        cells = [sb.tile([P, T], F32, name="cell%d" % t, align_bytes=64) for t in range(PACK)]
 
         nc.vector.memset(scale_table[:].bitcast(I32), 0)
         nc.vector.memset(warm[:, 0:1], 0.0)
@@ -58,8 +58,8 @@ def tile_picked_beamcell_none_po_kernel(
                 x_scales[0, r:16:4, :].bitcast(I32),
             )
         load_w("i", w2)
-        load_w("g", w3)
         load_w("f", w1)
+        load_w("g", w3)
         cell_rows = cell.rearrange("(p t) c -> p t c", t=PACK)
         for t in range(PACK):
             nc.sync.dma_start(cells[t][:], cell_rows[:, t, :])
@@ -120,13 +120,15 @@ def tile_picked_beamcell_none_po_kernel(
         deal(nc.scalar.copy, "i", 1, "staged1")
         for u in range(2):
             quantise("i", u)
-        let_in = [gate("i", t, ACT.Sigmoid, t) for t in range(3)]
+        let_in = [gate("i", t, ACT.Sigmoid, t) for t in range(PACK)]
+        prepare("f")
+        f0 = [
+            activate(product("f", 0, 4 + h, h * HALF, (h + 1) * HALF), ACT.Sigmoid, "f0_%d" % h) for h in range(2)
+        ]
+        keep = {t: gate("f", t, ACT.Sigmoid, (5 + t) % 8) for t in (1, 2, 3)}
         prepare("g")
-        new = {}
-        for t, bank in ((0, 3), (2, 4), (1, 3)):
-            new[t] = gate("g", t, ACT.Tanh, bank)
 
-        fresh = [sb.tile([P, S], F32, name="fresh%d" % t) for t in range(PACK)]
+        fresh = {}
         kept = [sb.tile([P, S], F32, name="kept%d" % t) for t in range(PACK)]
         y01 = sb.tile([P, 2, S], F32, name="y01")
         y23 = sb.tile([P, 2, S], F32, name="y23")
@@ -136,7 +138,8 @@ def tile_picked_beamcell_none_po_kernel(
         out_rows = out_0.rearrange("(p t) c -> p t c", t=PACK)
         out_words = out_1[0].rearrange("p n r -> p (n r)").bitcast(I32)
 
-        def make_fresh(t):
+        def make_fresh(t, tag):
+            fresh[t] = sb.tile([P, S], F32, name="fresh", tag=tag, align_bytes=64)
             nc.vector.tensor_tensor(fresh[t][:], let_in[t][:], new[t][:], MULT)
 
         def make_kept(t, c0, c1, factor=None):
@@ -151,34 +154,26 @@ def tile_picked_beamcell_none_po_kernel(
             y = (y01 if t < 2 else y23)[:, t % 2, c0:c1]
             nc.vector.tensor_tensor(y, kept[t][:, c0:c1], fresh[t][:, c0:c1], ADD)
 
-        deal(nc.vector.tensor_copy, "f", 0, "staged0")
-        make_fresh(0)
-        quantise("f", 0, "codes_g0")
-        make_fresh(2)
-        make_fresh(1)
-        f0 = [
-            activate(product("f", 0, bank, h * HALF, (h + 1) * HALF), ACT.Sigmoid, "f0_%d" % h)
-            for h, bank in enumerate((5, 7))
-        ]
-        acc_f1 = product("f", 1, 6)
-        deal(nc.scalar.copy, "f", 1, "codes_g0")
-        keep = {1: activate(acc_f1, ACT.Sigmoid, "f1")}
-        let_in.append(gate("i", 3, ACT.Sigmoid, 7))
-        new[3] = gate("g", 3, ACT.Tanh, 5)
+        new = {t: gate("g", t, ACT.Tanh, 1 + t) for t in range(3)}
         for h in range(2):
             make_kept(0, h * HALF, (h + 1) * HALF, f0[h])
-        add(0, 0, HALF)
-        add(0, HALF, S)
-        quantise("f", 1, "f0_1")
-        for t in (2, 3):
-            keep[t] = gate("f", t, ACT.Sigmoid, t - 2)
-        make_kept(1, 0, HALF)
-        make_kept(1, HALF, S)
+        make_fresh(0, "f0_0")
+        make_fresh(1, "fresh1")
+        add(0, 0, S)
+        make_fresh(2, "fresh2")
+        picked1 = sb.tile([P, S], F32, name="picked1")
+        for c0 in (0, HALF):
+            nc.scalar.activation(
+                picked1[:, c0 : c0 + HALF], cells[1][:].indirect(offsets[:, c0 // 16 : (c0 + HALF) // 16]), ACT.Copy
+            )
+        new[3] = activate(product("g", 3, 4), ACT.Tanh, "cell1")
+        for c0 in (0, HALF):
+            nc.vector.tensor_tensor(kept[1][:, c0 : c0 + HALF], picked1[:, c0 : c0 + HALF], keep[1][:, c0 : c0 + HALF], MULT)
         for c0 in (0, HALF):
             add(1, c0, c0 + HALF)
             nc.scalar.copy(y_bf[:, c0 : c0 + HALF, 0:2], y01[:, :, c0 : c0 + HALF].rearrange("p t c -> p c t"))
         nc.sync.dma_start(out_rows[:, 0:2, :], y01[:])
-        make_fresh(3)
+        make_fresh(3, "fresh3")
         make_kept(2, 0, HALF)
         make_kept(2, HALF, S)
 
@@ -198,51 +193,37 @@ def tile_picked_beamcell_none_po_kernel(
         add(2, HALF, S)
         nc.sync.dma_start(out_rows[:, 2, :], y23[:, 0, :])
         quarters = [slice(n * QUARTER, (n + 1) * QUARTER) for n in range(4)]
-        picked = sb.tile([P, 2, QUARTER], F32, name="picked")
+        kept_last = [kept[3][:, quarters[0]], kept[3][:, quarters[1]], keep[3][:, quarters[0]], keep[3][:, quarters[1]]]
 
-        def list_quarter(n):
-            return offsets[:, n * QUARTER // 16 : (n + 1) * QUARTER // 16]
-
-        def gather_times_keep(n):
-            nc.vector.tensor_tensor(kept[3][:, quarters[n]], cells[3][:].indirect(list_quarter(n)), keep[3][:, quarters[n]], MULT)
-
-        def gather_on_scalar(n):
-            nc.scalar.activation(picked[:, n - 1, :], cells[3][:].indirect(list_quarter(n)), ACT.Copy)
-
-        def times_keep(n):
-            nc.vector.tensor_tensor(kept[3][:, quarters[n]], picked[:, n - 1, :], keep[3][:, quarters[n]], MULT)
+        def gather_last(n):
+            nc.vector.tensor_tensor(
+                kept_last[n],
+                cells[3][:].indirect(offsets[:, n * QUARTER // 16 : (n + 1) * QUARTER // 16]),
+                keep[3][:, quarters[n]],
+                MULT,
+            )
 
         def add_last(n):
-            add(3, n * QUARTER, (n + 1) * QUARTER)
+            nc.vector.tensor_tensor(y23[:, 1, quarters[n]], kept_last[n], fresh[3][:, quarters[n]], ADD)
+            if n % 2 == 1:
+                nc.sync.dma_start(out_rows[:, 3, halves[n // 2]], y23[:, 1, halves[n // 2]])
 
-        def round_last(copy, n):
-            round_pair(copy, n * QUARTER, (n + 1) * QUARTER)
-
-        gather_on_scalar(1)
-        gather_on_scalar(2)
-        gather_times_keep(0)
-        gather_times_keep(3)
-        times_keep(1)
-        add_last(0)
-        round_last(nc.scalar.copy, 0)
-        times_keep(2)
-        add_last(1)
-        nc.sync.dma_start(out_rows[:, 3, halves[0]], y23[:, 1, halves[0]])
-        add_last(3)
-        round_last(nc.scalar.copy, 3)
-        add_last(2)
-        nc.sync.dma_start(out_rows[:, 3, halves[1]], y23[:, 1, halves[1]])
-        round_last(nc.vector.tensor_copy, 1)
-        round_last(nc.vector.tensor_copy, 2)
+        gather_last(0)
+        for n in range(3):
+            gather_last(n + 1)
+            add_last(n)
+            round_pair(nc.scalar.copy, n * QUARTER, (n + 1) * QUARTER)
         quantise_y(0)
+        add_last(3)
         quantise_y(1)
         nc.scalar.dma_start(out_words[:, halves[0]], y_codes[:, halves[0]].bitcast(I32))
+        round_pair(nc.vector.tensor_copy, 3 * QUARTER, S)
         quantise_y(2)
         quantise_y(3)
         nc.scalar.dma_start(out_words[:, halves[1]], y_codes[:, halves[1]].bitcast(I32))
         for q in range(4):
             queue = nc.scalar if q == 3 else nc.sync
             queue.dma_start(
-                out_2[0, 4 * q : 4 * q + 4, :].bitcast(I32),
-                y_scales[32 * q : 32 * q + 4, :].bitcast(I32),
+                out_2[0, q:16:4, :].bitcast(I32),
+                y_scales[q:P:32, :].bitcast(I32),
             )

@@ -195,13 +195,12 @@ def tile_picked_beamcell_none_po_kernel(
         quarters = [slice(n * QUARTER, (n + 1) * QUARTER) for n in range(4)]
         kept_last = [kept[3][:, quarters[0]], kept[3][:, quarters[1]], keep[3][:, quarters[0]], keep[3][:, quarters[1]]]
 
+        picked3 = sb.tile([P, QUARTER], F32, name="picked3")
+        nc.scalar.activation(picked3[:], cells[3][:].indirect(offsets[:, 3 * QUARTER // 16 :]), ACT.Copy)
+
         def gather_last(n):
-            nc.vector.tensor_tensor(
-                kept_last[n],
-                cells[3][:].indirect(offsets[:, n * QUARTER // 16 : (n + 1) * QUARTER // 16]),
-                keep[3][:, quarters[n]],
-                MULT,
-            )
+            source = picked3[:] if n == 3 else cells[3][:].indirect(offsets[:, n * QUARTER // 16 : (n + 1) * QUARTER // 16])
+            nc.vector.tensor_tensor(kept_last[n], source, keep[3][:, quarters[n]], MULT)
 
         def add_last(n):
             nc.vector.tensor_tensor(y23[:, 1, quarters[n]], kept_last[n], fresh[3][:, quarters[n]], ADD)
@@ -218,8 +217,8 @@ def tile_picked_beamcell_none_po_kernel(
         quantise_y(1)
         nc.scalar.dma_start(out_words[:, halves[0]], y_codes[:, halves[0]].bitcast(I32))
         round_pair(nc.vector.tensor_copy, 3 * QUARTER, S)
-        quantise_y(2)
         quantise_y(3)
+        quantise_y(2)
         nc.scalar.dma_start(out_words[:, halves[1]], y_codes[:, halves[1]].bitcast(I32))
         for q in range(4):
             queue = nc.scalar if q == 3 else nc.sync

@@ -98,8 +98,9 @@ def tile_picked_beamcell_none_po_kernel(
             )
             return acc
 
-        def activate(acc, func, tag):
-            value = sb.tile(list(acc.shape), F32, name="value", tag=tag, align_bytes=64)
+        def activate(acc, func, tag, value=None):
+            if value is None:
+                value = sb.tile(list(acc.shape), F32, name="value", tag=tag, align_bytes=64)
             nc.scalar.activation(value[:], acc[:], func)
             return value
 
@@ -122,17 +123,17 @@ def tile_picked_beamcell_none_po_kernel(
             quantise("i", u)
         let_in = [gate("i", t, ACT.Sigmoid, t) for t in range(PACK)]
         prepare("f")
-        f0 = [
-            activate(product("f", 0, 4 + h, h * HALF, (h + 1) * HALF), ACT.Sigmoid, "f0_%d" % h) for h in range(2)
-        ]
-        keep = {t: gate("f", t, ACT.Sigmoid, (5 + t) % 8) for t in (1, 2, 3)}
+        shared = sb.tile([P, 2 * S - QUARTER], F32, name="shared", align_bytes=64)
+        keep = {
+            t: activate(product("f", t, 4 + t), ACT.Sigmoid, "f%d" % t, shared[:, S - QUARTER :] if t == 2 else None)
+            for t in range(PACK)
+        }
         prepare("g")
 
         fresh = {}
         kept = [sb.tile([P, S], F32, name="kept%d" % t) for t in range(PACK)]
         y01 = sb.tile([P, 2, S], F32, name="y01")
         y23 = sb.tile([P, 2, S], F32, name="y23")
-        y_bf = sb.tile([P, S, PACK], BF16, name="y_bf", align_bytes=64)
         y_codes = sb.tile([P, S], U32, name="y_codes", align_bytes=64)
         y_scales = sb.tile([P, S], U8, name="y_scales", align_bytes=64)
         out_rows = out_0.rearrange("(p t) c -> p t c", t=PACK)
@@ -154,10 +155,9 @@ def tile_picked_beamcell_none_po_kernel(
             y = (y01 if t < 2 else y23)[:, t % 2, c0:c1]
             nc.vector.tensor_tensor(y, kept[t][:, c0:c1], fresh[t][:, c0:c1], ADD)
 
-        new = {t: gate("g", t, ACT.Tanh, 1 + t) for t in range(3)}
-        for h in range(2):
-            make_kept(0, h * HALF, (h + 1) * HALF, f0[h])
-        make_fresh(0, "f0_0")
+        new = {t: gate("g", t, ACT.Tanh, t) for t in range(3)}
+        make_kept(0, 0, S)
+        make_fresh(0, "fresh0")
         make_fresh(1, "fresh1")
         add(0, 0, S)
         make_fresh(2, "fresh2")
@@ -166,16 +166,22 @@ def tile_picked_beamcell_none_po_kernel(
             nc.scalar.activation(
                 picked1[:, c0 : c0 + HALF], cells[1][:].indirect(offsets[:, c0 // 16 : (c0 + HALF) // 16]), ACT.Copy
             )
-        new[3] = activate(product("g", 3, 4), ACT.Tanh, "cell1")
+        new[3] = activate(product("g", 3, 3), ACT.Tanh, "cell1")
         for c0 in (0, HALF):
             nc.vector.tensor_tensor(kept[1][:, c0 : c0 + HALF], picked1[:, c0 : c0 + HALF], keep[1][:, c0 : c0 + HALF], MULT)
         for c0 in (0, HALF):
             add(1, c0, c0 + HALF)
-            nc.scalar.copy(y_bf[:, c0 : c0 + HALF, 0:2], y01[:, :, c0 : c0 + HALF].rearrange("p t c -> p c t"))
         nc.sync.dma_start(out_rows[:, 0:2, :], y01[:])
-        make_fresh(3, "fresh3")
-        make_kept(2, 0, HALF)
-        make_kept(2, HALF, S)
+        picked2 = sb.tile([P, HALF], F32, name="picked2")
+        nc.scalar.activation(picked2[:], cells[2][:].indirect(offsets[:, HALF // 16 :]), ACT.Copy)
+        make_kept(2, 0, QUARTER)
+        make_kept(2, QUARTER, HALF)
+        y_bf = sb.tile([P, S, PACK], BF16, name="y_bf", tag="cell2", align_bytes=64)
+        for c0 in (0, HALF):
+            nc.scalar.copy(y_bf[:, c0 : c0 + HALF, 0:2], y01[:, :, c0 : c0 + HALF].rearrange("p t c -> p c t"))
+        fresh[3] = shared[:, :S]
+        nc.vector.tensor_tensor(fresh[3], let_in[3][:], new[3][:], MULT)
+        nc.vector.tensor_tensor(kept[2][:, HALF:], picked2[:], keep[2][:, HALF:], MULT)
 
         def round_pair(copy, c0, c1):
             copy(y_bf[:, c0:c1, 2:4], y23[:, :, c0:c1].rearrange("p t c -> p c t"))
@@ -211,14 +217,16 @@ def tile_picked_beamcell_none_po_kernel(
         for n in range(3):
             gather_last(n + 1)
             add_last(n)
-            round_pair(nc.scalar.copy, n * QUARTER, (n + 1) * QUARTER)
-        quantise_y(0)
+            if n < 2:
+                round_pair(nc.scalar.copy, n * QUARTER, (n + 1) * QUARTER)
         add_last(3)
+        round_pair(nc.vector.tensor_copy, 2 * QUARTER, 3 * QUARTER)
+        quantise_y(0)
+        round_pair(nc.vector.tensor_copy, 3 * QUARTER, S)
         quantise_y(1)
         nc.scalar.dma_start(out_words[:, halves[0]], y_codes[:, halves[0]].bitcast(I32))
-        round_pair(nc.vector.tensor_copy, 3 * QUARTER, S)
-        quantise_y(3)
         quantise_y(2)
+        quantise_y(3)
         nc.scalar.dma_start(out_words[:, halves[1]], y_codes[:, halves[1]].bitcast(I32))
         for q in range(4):
             queue = nc.scalar if q == 3 else nc.sync

@@ -58,8 +58,8 @@ def tile_picked_beamcell_none_po_kernel(
                 x_scales[0, r:16:4, :].bitcast(I32),
             )
         load_w("i", w2)
-        load_w("f", w1)
         load_w("g", w3)
+        load_w("f", w1)
         cell_rows = cell.rearrange("(p t) c -> p t c", t=PACK)
         for t in range(PACK):
             nc.sync.dma_start(cells[t][:], cell_rows[:, t, :])
@@ -122,13 +122,9 @@ def tile_picked_beamcell_none_po_kernel(
         for u in range(2):
             quantise("i", u)
         let_in = [gate("i", t, ACT.Sigmoid, t) for t in range(PACK)]
-        prepare("f")
-        shared = sb.tile([P, 2 * S - QUARTER], F32, name="shared", align_bytes=64)
-        keep = {
-            t: activate(product("f", t, 4 + t), ACT.Sigmoid, "f%d" % t, shared[:, S - QUARTER :] if t == 2 else None)
-            for t in range(PACK)
-        }
         prepare("g")
+        new = [gate("g", t, ACT.Tanh, 4 + t) for t in range(PACK)]
+        prepare("f")
 
         fresh = {}
         kept = [sb.tile([P, S], F32, name="kept%d" % t) for t in range(PACK)]
@@ -155,33 +151,32 @@ def tile_picked_beamcell_none_po_kernel(
             y = (y01 if t < 2 else y23)[:, t % 2, c0:c1]
             nc.vector.tensor_tensor(y, kept[t][:, c0:c1], fresh[t][:, c0:c1], ADD)
 
-        new = {t: gate("g", t, ACT.Tanh, t) for t in range(3)}
-        make_kept(0, 0, S)
-        make_fresh(0, "fresh0")
-        make_fresh(1, "fresh1")
-        add(0, 0, S)
-        make_fresh(2, "fresh2")
-        picked1 = sb.tile([P, S], F32, name="picked1")
+        keep = {t: gate("f", t, ACT.Sigmoid, t) for t in range(2)}
+        for t in range(3):
+            make_fresh(t, "fresh%d" % t)
+        make_kept(0, 0, HALF)
+        make_fresh(3, "fresh3")
+        picked0 = sb.tile([P, HALF], F32, name="picked0")
+        nc.scalar.activation(picked0[:], cells[0][:].indirect(offsets[:, HALF // 16 :]), ACT.Copy)
+        nc.vector.tensor_tensor(kept[0][:, HALF:], picked0[:], keep[0][:, HALF:], MULT)
+        for c0 in (0, HALF):
+            add(0, c0, c0 + HALF)
+        picked1 = sb.tile([P, S], F32, name="picked1", align_bytes=64)
         for c0 in (0, HALF):
             nc.scalar.activation(
                 picked1[:, c0 : c0 + HALF], cells[1][:].indirect(offsets[:, c0 // 16 : (c0 + HALF) // 16]), ACT.Copy
             )
-        new[3] = activate(product("g", 3, 3), ACT.Tanh, "cell1")
+        keep[2] = activate(product("f", 2, 2), ACT.Sigmoid, "cell1")
         for c0 in (0, HALF):
             nc.vector.tensor_tensor(kept[1][:, c0 : c0 + HALF], picked1[:, c0 : c0 + HALF], keep[1][:, c0 : c0 + HALF], MULT)
+        keep[3] = activate(product("f", 3, 3), ACT.Sigmoid, "picked1")
+        y_bf = sb.tile([P, S, PACK], BF16, name="y_bf", align_bytes=64)
         for c0 in (0, HALF):
             add(1, c0, c0 + HALF)
-        nc.sync.dma_start(out_rows[:, 0:2, :], y01[:])
-        picked2 = sb.tile([P, HALF], F32, name="picked2")
-        nc.scalar.activation(picked2[:], cells[2][:].indirect(offsets[:, HALF // 16 :]), ACT.Copy)
-        make_kept(2, 0, QUARTER)
-        make_kept(2, QUARTER, HALF)
-        y_bf = sb.tile([P, S, PACK], BF16, name="y_bf", tag="cell2", align_bytes=64)
-        for c0 in (0, HALF):
             nc.scalar.copy(y_bf[:, c0 : c0 + HALF, 0:2], y01[:, :, c0 : c0 + HALF].rearrange("p t c -> p c t"))
-        fresh[3] = shared[:, :S]
-        nc.vector.tensor_tensor(fresh[3], let_in[3][:], new[3][:], MULT)
-        nc.vector.tensor_tensor(kept[2][:, HALF:], picked2[:], keep[2][:, HALF:], MULT)
+        nc.sync.dma_start(out_rows[:, 0:2, :], y01[:])
+        make_kept(2, 0, HALF)
+        make_kept(2, HALF, S)
 
         def round_pair(copy, c0, c1):
             copy(y_bf[:, c0:c1, 2:4], y23[:, :, c0:c1].rearrange("p t c -> p c t"))
@@ -199,17 +194,18 @@ def tile_picked_beamcell_none_po_kernel(
         add(2, HALF, S)
         nc.sync.dma_start(out_rows[:, 2, :], y23[:, 0, :])
         quarters = [slice(n * QUARTER, (n + 1) * QUARTER) for n in range(4)]
-        kept_last = [kept[3][:, quarters[0]], kept[3][:, quarters[1]], keep[3][:, quarters[0]], keep[3][:, quarters[1]]]
-
-        picked3 = sb.tile([P, QUARTER], F32, name="picked3")
-        nc.scalar.activation(picked3[:], cells[3][:].indirect(offsets[:, 3 * QUARTER // 16 :]), ACT.Copy)
+        picked3 = sb.tile([P, HALF], F32, name="picked3")
+        for n in (2, 3):
+            nc.scalar.activation(
+                picked3[:, quarters[n - 2]], cells[3][:].indirect(offsets[:, n * QUARTER // 16 : (n + 1) * QUARTER // 16]), ACT.Copy
+            )
 
         def gather_last(n):
-            source = picked3[:] if n == 3 else cells[3][:].indirect(offsets[:, n * QUARTER // 16 : (n + 1) * QUARTER // 16])
-            nc.vector.tensor_tensor(kept_last[n], source, keep[3][:, quarters[n]], MULT)
+            source = picked3[:, quarters[n - 2]] if n >= 2 else cells[3][:].indirect(offsets[:, n * QUARTER // 16 : (n + 1) * QUARTER // 16])
+            nc.vector.tensor_tensor(kept[3][:, quarters[n]], source, keep[3][:, quarters[n]], MULT)
 
         def add_last(n):
-            nc.vector.tensor_tensor(y23[:, 1, quarters[n]], kept_last[n], fresh[3][:, quarters[n]], ADD)
+            nc.vector.tensor_tensor(y23[:, 1, quarters[n]], kept[3][:, quarters[n]], fresh[3][:, quarters[n]], ADD)
             if n % 2 == 1:
                 nc.sync.dma_start(out_rows[:, 3, halves[n // 2]], y23[:, 1, halves[n // 2]])
 

@@ -32,14 +32,11 @@ def tile_picked_beamcell_none_po_kernel(
 
         offsets = sb.tile([P, S // 16], U16, name="offsets")
         word_table = sb.tile([P, T], U32, name="word_table", tag="staged1", align_bytes=64)
-        scale_table = sb.tile([P, T], U8, name="scale_table", tag="staged0", align_bytes=64)
         warm = sb.tile([P, 2], F32, name="warm")
-        raw = {}
-        for name in ("i", "g", "f"):
-            raw[name] = sb.tile([P, PACK, N], F32, name="raw_" + name)
-        cells = [sb.tile([P, T], F32, name="cell%d" % t, align_bytes=64) for t in range(PACK)]
+        raw = {"i": sb.tile([P, PACK, N], F32, name="raw_i")}
+        x_bytes = sb.tile([P, S], U8, name="x_bytes", align_bytes=64)
+        x_codes = sb.tile([P, S], U32, name="x_codes", align_bytes=64)
 
-        nc.vector.memset(scale_table[:].bitcast(I32), 0)
         nc.vector.memset(warm[:, 0:1], 0.0)
         nc.scalar.activation(warm[:, 1:2], warm[:, 0:1], ACT.Sigmoid)
 
@@ -49,15 +46,23 @@ def tile_picked_beamcell_none_po_kernel(
             )
 
         word_rows = x_words[0].rearrange("p n r -> p (n r)").bitcast(I32)
-        for c0 in (0, T // 2):
-            nc.sync.dma_start(word_table[:, c0 : c0 + T // 2].bitcast(I32), word_rows[:, c0 : c0 + T // 2])
-        nc.sync.dma_start(offsets[:], offs)
-        for r in range(4):
-            nc.sync.dma_start(
-                scale_table[r:P:32, :].bitcast(I32),
-                x_scales[0, r:16:4, :].bitcast(I32),
-            )
-        load_w("i", w2)
+        with tc.tile_pool(name="early", bufs=1) as early:
+            scale_table = early.tile([P, T], U8, name="scale_table", align_bytes=64)
+            nc.vector.memset(scale_table[:].bitcast(I32), 0)
+            nc.sync.dma_start(word_table[:, : T // 8].bitcast(I32), word_rows[:, : T // 8])
+            nc.sync.dma_start(offsets[:], offs)
+            nc.sync.dma_start(scale_table[0:P:8, :].bitcast(I32), x_scales[0].bitcast(I32))
+            nc.sync.dma_start(word_table[:, T // 8 :].bitcast(I32), word_rows[:, T // 8 :])
+            load_w("i", w2)
+            picked_bytes = early.tile([P, S], U8, name="picked_bytes", align_bytes=64)
+            nc.vector.tensor_copy(picked_bytes[:], scale_table[:].indirect(offsets[:]))
+            nc.vector.tensor_copy(x_bytes[:].bitcast(I32), picked_bytes[:].bitcast(I32))
+        for r in range(1, 4):
+            nc.sync.dma_start(x_bytes[r:P:32, :].bitcast(I32), x_bytes[8 * r : P : 32, :].bitcast(I32))
+        late = ctx.enter_context(tc.tile_pool(name="late", bufs=1))
+        for name in ("g", "f"):
+            raw[name] = late.tile([P, PACK, N], F32, name="raw_" + name)
+        cells = [late.tile([P, T], F32, name="cell%d" % t, align_bytes=64) for t in range(PACK)]
         load_w("g", w3)
         load_w("f", w1)
         cell_rows = cell.rearrange("(p t) c -> p t c", t=PACK)
@@ -98,9 +103,8 @@ def tile_picked_beamcell_none_po_kernel(
             )
             return acc
 
-        def activate(acc, func, tag, value=None):
-            if value is None:
-                value = sb.tile(list(acc.shape), F32, name="value", tag=tag, align_bytes=64)
+        def activate(acc, func, tag, pool=sb):
+            value = pool.tile(list(acc.shape), F32, name="value", tag=tag, align_bytes=64)
             nc.scalar.activation(value[:], acc[:], func)
             return value
 
@@ -113,10 +117,7 @@ def tile_picked_beamcell_none_po_kernel(
             for u in range(2):
                 quantise(name, u)
 
-        x_bytes = sb.tile([P, S], U8, name="x_bytes", align_bytes=64)
-        x_codes = sb.tile([P, S], U32, name="x_codes", align_bytes=64)
         nc.vector.tensor_copy(x_codes[:], word_table[:].indirect(offsets[:]))
-        nc.vector.tensor_copy(x_bytes[:], scale_table[:].indirect(offsets[:]))
         deal(nc.vector.tensor_copy, "i", 0, "staged0")
         deal(nc.scalar.copy, "i", 1, "staged1")
         for u in range(2):
@@ -166,7 +167,7 @@ def tile_picked_beamcell_none_po_kernel(
             nc.scalar.activation(
                 picked1[:, c0 : c0 + HALF], cells[1][:].indirect(offsets[:, c0 // 16 : (c0 + HALF) // 16]), ACT.Copy
             )
-        keep[2] = activate(product("f", 2, 2), ACT.Sigmoid, "cell1")
+        keep[2] = activate(product("f", 2, 2), ACT.Sigmoid, "cell1", late)
         for c0 in (0, HALF):
             nc.vector.tensor_tensor(kept[1][:, c0 : c0 + HALF], picked1[:, c0 : c0 + HALF], keep[1][:, c0 : c0 + HALF], MULT)
         keep[3] = activate(product("f", 3, 3), ACT.Sigmoid, "picked1")

@@ -211,15 +211,18 @@ def tile_picked_beamcell_none_po_kernel(
                 nc.sync.dma_start(out_rows[:, 3, halves[n // 2]], y23[:, 1, halves[n // 2]])
 
         gather_last(0)
-        for n in range(3):
-            gather_last(n + 1)
-            add_last(n)
-            if n < 2:
-                round_pair(nc.scalar.copy, n * QUARTER, (n + 1) * QUARTER)
+        gather_last(1)
+        add_last(0)
+        round_pair(nc.scalar.copy, 0 * QUARTER, 1 * QUARTER)
+        gather_last(2)
+        add_last(1)
+        round_pair(nc.scalar.copy, 1 * QUARTER, 2 * QUARTER)
+        gather_last(3)
+        add_last(2)
         add_last(3)
+        round_pair(nc.scalar.copy, 3 * QUARTER, 4 * QUARTER)
         round_pair(nc.vector.tensor_copy, 2 * QUARTER, 3 * QUARTER)
         quantise_y(0)
-        round_pair(nc.vector.tensor_copy, 3 * QUARTER, S)
         quantise_y(1)
         nc.scalar.dma_start(out_words[:, halves[0]], y_codes[:, halves[0]].bitcast(I32))
         quantise_y(2)

@@ -37,9 +37,6 @@ def tile_picked_beamcell_none_po_kernel(
         x_bytes = sb.tile([P, S], U8, name="x_bytes", align_bytes=64)
         x_codes = sb.tile([P, S], U32, name="x_codes", align_bytes=64)
 
-        nc.vector.memset(warm[:, 0:1], 0.0)
-        nc.scalar.activation(warm[:, 1:2], warm[:, 0:1], ACT.Sigmoid)
-
         def load_w(name, w):
             nc.sync.dma_start(
                 raw[name][:].rearrange("p j c -> p (j c)"), w.rearrange("(p j) c -> p (j c)", j=PACK)
@@ -49,6 +46,8 @@ def tile_picked_beamcell_none_po_kernel(
         with tc.tile_pool(name="early", bufs=1) as early:
             scale_table = early.tile([P, T], U8, name="scale_table", align_bytes=64)
             nc.vector.memset(scale_table[:].bitcast(I32), 0)
+            nc.vector.memset(warm[:, 0:1], 0.0)
+            nc.scalar.activation(warm[:, 1:2], warm[:, 0:1], ACT.Sigmoid)
             nc.sync.dma_start(word_table[:, : T // 8].bitcast(I32), word_rows[:, : T // 8])
             nc.sync.dma_start(offsets[:], offs)
             nc.sync.dma_start(scale_table[0:P:8, :].bitcast(I32), x_scales[0].bitcast(I32))
@@ -129,8 +128,8 @@ def tile_picked_beamcell_none_po_kernel(
 
         fresh = {}
         kept = [sb.tile([P, S], F32, name="kept%d" % t) for t in range(PACK)]
-        y01 = sb.tile([P, 2, S], F32, name="y01")
-        y23 = sb.tile([P, 2, S], F32, name="y23")
+        y = sb.tile([P, PACK, S], F32, name="y")
+        y01, y23 = y[:, 0:2, :], y[:, 2:4, :]
         y_codes = sb.tile([P, S], U32, name="y_codes", align_bytes=64)
         y_scales = sb.tile([P, S], U8, name="y_scales", align_bytes=64)
         out_rows = out_0.rearrange("(p t) c -> p t c", t=PACK)
@@ -149,8 +148,7 @@ def tile_picked_beamcell_none_po_kernel(
             )
 
         def add(t, c0, c1):
-            y = (y01 if t < 2 else y23)[:, t % 2, c0:c1]
-            nc.vector.tensor_tensor(y, kept[t][:, c0:c1], fresh[t][:, c0:c1], ADD)
+            nc.vector.tensor_tensor(y[:, t, c0:c1], kept[t][:, c0:c1], fresh[t][:, c0:c1], ADD)
 
         keep = {t: gate("f", t, ACT.Sigmoid, t) for t in range(2)}
         for t in range(3):
@@ -174,7 +172,9 @@ def tile_picked_beamcell_none_po_kernel(
         y_bf = sb.tile([P, S, PACK], BF16, name="y_bf", align_bytes=64)
         for c0 in (0, HALF):
             add(1, c0, c0 + HALF)
-            nc.scalar.copy(y_bf[:, c0 : c0 + HALF, 0:2], y01[:, :, c0 : c0 + HALF].rearrange("p t c -> p c t"))
+            c1 = c0 + HALF
+            c0 = c0 + QUARTER if c0 else c0
+            nc.scalar.copy(y_bf[:, c0:c1, 0:2], y01[:, :, c0:c1].rearrange("p t c -> p c t"))
         nc.sync.dma_start(out_rows[:, 0:2, :], y01[:])
         make_kept(2, 0, HALF)
         make_kept(2, HALF, S)
@@ -221,7 +221,10 @@ def tile_picked_beamcell_none_po_kernel(
         add_last(2)
         add_last(3)
         round_pair(nc.scalar.copy, 3 * QUARTER, 4 * QUARTER)
-        round_pair(nc.vector.tensor_copy, 2 * QUARTER, 3 * QUARTER)
+        nc.vector.tensor_copy(
+            y_bf[:, quarters[2], :].rearrange("p (c i) t -> p c t i", i=4),
+            y[:, :, quarters[2]].rearrange("p t (c i) -> p c t i", i=4),
+        )
         quantise_y(0)
         quantise_y(1)
         nc.scalar.dma_start(out_words[:, halves[0]], y_codes[:, halves[0]].bitcast(I32))

from contextlib import ExitStack

import concourse.mybir as mybir

K, T, S, N = 512, 2048, 512, 512
FLOPS = 3 * 2 * K * N * S

F32 = mybir.dt.float32
BF16 = mybir.dt.bfloat16
I32 = mybir.dt.int32
U32 = mybir.dt.uint32
U16 = mybir.dt.uint16
U8 = mybir.dt.uint8
FP8X4 = mybir.dt.float8_e4m3fn_x4
ACT = mybir.ActivationFunctionType
MULT = mybir.AluOpType.mult
ADD = mybir.AluOpType.add

P = 128
PACK = 4
HALF = S // 2
QUARTER = S // 4


def tile_picked_beamcell_none_po_kernel(
    tc, x_words, x_scales, w1, w2, w3, cell, offs, out_0, out_1, out_2
):
    nc = tc.nc
    with ExitStack() as ctx:
        sb = ctx.enter_context(tc.tile_pool(name="sb", bufs=1))
        psum = ctx.enter_context(tc.psum_pool(name="psum", bufs=1))

        offsets = sb.tile([P, S // 16], U16, name="offsets")
        word_table = sb.tile([P, T], U32, name="word_table", tag="staged1", align_bytes=64)
        warm = sb.tile([P, 2], F32, name="warm")
        raw = {"i": sb.tile([P, PACK, N], F32, name="raw_i")}
        x_bytes = sb.tile([P, S], U8, name="x_bytes", align_bytes=64)
        x_codes = sb.tile([P, S], U32, name="x_codes", align_bytes=64)

        def load_w(name, w):
            nc.sync.dma_start(
                raw[name][:].rearrange("p j c -> p (j c)"), w.rearrange("(p j) c -> p (j c)", j=PACK)
            )

        word_rows = x_words[0].rearrange("p n r -> p (n r)").bitcast(I32)
        with tc.tile_pool(name="early", bufs=1) as early:
            scale_table = early.tile([P, T], U8, name="scale_table", align_bytes=64)
            nc.vector.memset(scale_table[:].bitcast(I32), 0)
            nc.vector.memset(warm[:, 0:1], 0.0)
            nc.scalar.activation(warm[:, 1:2], warm[:, 0:1], ACT.Sigmoid)
            nc.sync.dma_start(word_table[:, : T // 8].bitcast(I32), word_rows[:, : T // 8])
            nc.sync.dma_start(offsets[:], offs)
            nc.sync.dma_start(scale_table[0:P:8, :].bitcast(I32), x_scales[0].bitcast(I32))
            nc.sync.dma_start(word_table[:, T // 8 :].bitcast(I32), word_rows[:, T // 8 :])
            load_w("i", w2)
            picked_bytes = early.tile([P, S], U8, name="picked_bytes", align_bytes=64)
            nc.vector.tensor_copy(picked_bytes[:], scale_table[:].indirect(offsets[:]))
            nc.vector.tensor_copy(x_bytes[:].bitcast(I32), picked_bytes[:].bitcast(I32))
        for r in range(1, 4):
            nc.sync.dma_start(x_bytes[r:P:32, :].bitcast(I32), x_bytes[8 * r : P : 32, :].bitcast(I32))
        late = ctx.enter_context(tc.tile_pool(name="late", bufs=1))
        for name in ("g", "f"):
            raw[name] = late.tile([P, PACK, N], F32, name="raw_" + name)
        cells = [late.tile([P, T], F32, name="cell%d" % t, align_bytes=64) for t in range(PACK)]
        load_w("g", w3)
        load_w("f", w1)
        cell_rows = cell.rearrange("(p t) c -> p t c", t=PACK)
        for t in range(PACK):
            nc.sync.dma_start(cells[t][:], cell_rows[:, t, :])

        staged, codes, scales = {}, {}, {}

        def deal(copy, name, u, tag):
            staged[name, u] = sb.tile([P, 2, P, PACK], BF16, name="staged", tag=tag, align_bytes=64)
            copy(
                staged[name, u][:].rearrange("p t m j -> p m j t"),
                raw[name][:].rearrange("p j (m t) -> p m j t", t=PACK)[:, :, :, 2 * u : 2 * u + 2],
            )

        def quantise(name, u, tag=None):
            codes[name, u] = sb.tile(
                [P, 2 * P], U32, name="codes", tag=tag or "codes_%s%d" % (name, u), align_bytes=64
            )
            scales[name, u] = sb.tile([P, 2 * P], U8, name="scales_%s%d" % (name, u), align_bytes=64)
            nc.vector.quantize_mx(
                out=codes[name, u][:].bitcast(FP8X4),
                scales=scales[name, u][:],
                in_=staged[name, u][:].rearrange("p t m j -> p (t m j)"),
            )

        def product(name, t, bank, c0=0, c1=S):
            cols = slice(P * (t % 2), P * (t % 2 + 1))
            acc = psum.tile([P, c1 - c0], F32, name="acc", tag="bank%d" % bank)
            nc.tensor.matmul_mx(
                out=acc[:],
                lhsT=codes[name, t // 2][:, cols].bitcast(FP8X4),
                lhsT_scale=scales[name, t // 2][:, cols],
                rhs=x_codes[:, c0:c1].bitcast(FP8X4),
                rhs_scale=x_bytes[:, c0:c1],
                start=True,
                stop=True,
            )
            return acc

        def activate(acc, func, tag, pool=sb):
            value = pool.tile(list(acc.shape), F32, name="value", tag=tag, align_bytes=64)
            nc.scalar.activation(value[:], acc[:], func)
            return value

        def gate(name, t, func, bank):
            return activate(product(name, t, bank), func, "%s%d" % (name, t))

        def prepare(name):
            for u in range(2):
                deal(nc.vector.tensor_copy, name, u, "staged%d" % u)
            for u in range(2):
                quantise(name, u)

        nc.vector.tensor_copy(x_codes[:], word_table[:].indirect(offsets[:]))
        deal(nc.vector.tensor_copy, "i", 0, "staged0")
        deal(nc.scalar.copy, "i", 1, "staged1")
        for u in range(2):
            quantise("i", u)
        let_in = [gate("i", t, ACT.Sigmoid, t) for t in range(PACK)]
        prepare("g")
        new = [gate("g", t, ACT.Tanh, 4 + t) for t in range(PACK)]
        prepare("f")

        fresh = {}
        kept = [sb.tile([P, S], F32, name="kept%d" % t) for t in range(PACK)]
        y = sb.tile([P, PACK, S], F32, name="y")
        y01, y23 = y[:, 0:2, :], y[:, 2:4, :]
        y_codes = sb.tile([P, S], U32, name="y_codes", align_bytes=64)
        y_scales = sb.tile([P, S], U8, name="y_scales", align_bytes=64)
        out_rows = out_0.rearrange("(p t) c -> p t c", t=PACK)
        out_words = out_1[0].rearrange("p n r -> p (n r)").bitcast(I32)

        def make_fresh(t, tag):
            fresh[t] = sb.tile([P, S], F32, name="fresh", tag=tag, align_bytes=64)
            nc.vector.tensor_tensor(fresh[t][:], let_in[t][:], new[t][:], MULT)

        def make_kept(t, c0, c1, factor=None):
            nc.vector.tensor_tensor(
                kept[t][:, c0:c1],
                cells[t][:].indirect(offsets[:, c0 // 16 : c1 // 16]),
                keep[t][:, c0:c1] if factor is None else factor[:],
                MULT,
            )

        def add(t, c0, c1):
            nc.vector.tensor_tensor(y[:, t, c0:c1], kept[t][:, c0:c1], fresh[t][:, c0:c1], ADD)

        keep = {t: gate("f", t, ACT.Sigmoid, t) for t in range(2)}
        for t in range(3):
            make_fresh(t, "fresh%d" % t)
        make_kept(0, 0, HALF)
        make_fresh(3, "fresh3")
        picked0 = sb.tile([P, HALF], F32, name="picked0")
        nc.scalar.activation(picked0[:], cells[0][:].indirect(offsets[:, HALF // 16 :]), ACT.Copy)
        nc.vector.tensor_tensor(kept[0][:, HALF:], picked0[:], keep[0][:, HALF:], MULT)
        for c0 in (0, HALF):
            add(0, c0, c0 + HALF)
        picked1 = sb.tile([P, S], F32, name="picked1", align_bytes=64)
        for c0 in (0, HALF):
            nc.scalar.activation(
                picked1[:, c0 : c0 + HALF], cells[1][:].indirect(offsets[:, c0 // 16 : (c0 + HALF) // 16]), ACT.Copy
            )
        keep[2] = activate(product("f", 2, 2), ACT.Sigmoid, "cell1", late)
        for c0 in (0, HALF):
            nc.vector.tensor_tensor(kept[1][:, c0 : c0 + HALF], picked1[:, c0 : c0 + HALF], keep[1][:, c0 : c0 + HALF], MULT)
        keep[3] = activate(product("f", 3, 3), ACT.Sigmoid, "picked1")
        y_bf = sb.tile([P, S, PACK], BF16, name="y_bf", align_bytes=64)
        for c0 in (0, HALF):
            add(1, c0, c0 + HALF)
            c1 = c0 + HALF
            c0 = c0 + QUARTER if c0 else c0
            nc.scalar.copy(y_bf[:, c0:c1, 0:2], y01[:, :, c0:c1].rearrange("p t c -> p c t"))
        nc.sync.dma_start(out_rows[:, 0:2, :], y01[:])
        make_kept(2, 0, HALF)
        make_kept(2, HALF, S)

        def round_pair(copy, c0, c1):
            copy(y_bf[:, c0:c1, 2:4], y23[:, :, c0:c1].rearrange("p t c -> p c t"))

        def quantise_y(n):
            cols = slice(n * QUARTER, (n + 1) * QUARTER)
            nc.vector.quantize_mx(
                out=y_codes[:, cols].bitcast(FP8X4),
                scales=y_scales[:, cols],
                in_=y_bf[:, cols, :].rearrange("p c t -> p (c t)"),
            )

        halves = [slice(h * HALF, (h + 1) * HALF) for h in range(2)]
        add(2, 0, HALF)
        add(2, HALF, S)
        nc.sync.dma_start(out_rows[:, 2, :], y23[:, 0, :])
        quarters = [slice(n * QUARTER, (n + 1) * QUARTER) for n in range(4)]
        picked3 = sb.tile([P, HALF], F32, name="picked3")
        for n in (2, 3):
            nc.scalar.activation(
                picked3[:, quarters[n - 2]], cells[3][:].indirect(offsets[:, n * QUARTER // 16 : (n + 1) * QUARTER // 16]), ACT.Copy
            )

        def gather_last(n):
            source = picked3[:, quarters[n - 2]] if n >= 2 else cells[3][:].indirect(offsets[:, n * QUARTER // 16 : (n + 1) * QUARTER // 16])
            nc.vector.tensor_tensor(kept[3][:, quarters[n]], source, keep[3][:, quarters[n]], MULT)

        def add_last(n):
            nc.vector.tensor_tensor(y23[:, 1, quarters[n]], kept[3][:, quarters[n]], fresh[3][:, quarters[n]], ADD)
            if n % 2 == 1:
                nc.sync.dma_start(out_rows[:, 3, halves[n // 2]], y23[:, 1, halves[n // 2]])

        gather_last(0)
        gather_last(1)
        add_last(0)
        round_pair(nc.scalar.copy, 0 * QUARTER, 1 * QUARTER)
        gather_last(2)
        add_last(1)
        round_pair(nc.scalar.copy, 1 * QUARTER, 2 * QUARTER)
        gather_last(3)
        add_last(2)
        add_last(3)
        round_pair(nc.scalar.copy, 3 * QUARTER, 4 * QUARTER)
        nc.vector.tensor_copy(
            y_bf[:, quarters[2], :].rearrange("p (c i) t -> p c t i", i=4),
            y[:, :, quarters[2]].rearrange("p t (c i) -> p c t i", i=4),
        )
        quantise_y(0)
        quantise_y(1)
        nc.scalar.dma_start(out_words[:, halves[0]], y_codes[:, halves[0]].bitcast(I32))
        quantise_y(2)
        quantise_y(3)
        nc.scalar.dma_start(out_words[:, halves[1]], y_codes[:, halves[1]].bitcast(I32))
        for q in range(4):
            queue = nc.scalar if q == 3 else nc.sync
            queue.dma_start(
                out_2[0, q:16:4, :].bitcast(I32),
                y_scales[q:P:32, :].bitcast(I32),
            )
